import numpy as np, ml_dtypes
CORES = [3,7,11,15,131,135,139,143]
N = 8
import mx_ref
BF = ml_dtypes.bfloat16
def gentries(a):
    return np.ascontiguousarray(a.reshape(8, 16, -1).transpose(0, 2, 1)).reshape(8, -1)
def gtable(e):
    e = np.asarray(e); return np.ascontiguousarray(e.reshape(8, -1, 16).transpose(0, 2, 1)).reshape(128, -1).astype(np.int32)
def gcols(t, e):
    v = np.concatenate([t.reshape(8, 16, -1, 4), np.zeros((8, 16, 1, 4), BF)], axis=2)
    return np.ascontiguousarray(np.stack([v[g][:, e[g]] for g in range(8)])).reshape(128, -1)
def tile(rs):
    return np.stack(rs, axis=2).reshape(128, -1).astype(BF)
def pick(q, e):
    c = np.concatenate([q[0].reshape(128, -1, 4), np.zeros((128, 1, 4), np.uint8)], axis=1); s = np.concatenate([q[1], np.ones((16, 1), np.uint8)], axis=1)
    return (np.ascontiguousarray(c[:, e].reshape(128, -1)), np.ascontiguousarray(s[:, e]))
def join(*qs):
    return (np.concatenate([q[0] for q in qs], axis=1), np.concatenate([q[1] for q in qs], axis=1))
def put(q, e, v):
    c, s = q[0].reshape(128, -1, 4).copy(), q[1].copy(); c[:, e] = v[0].reshape(128, -1, 4); s[:, e] = v[1]
    return (c.reshape(128, -1), s)
def pk(c, s):
    return (np.ascontiguousarray(c), mx_ref.live(s))
def emit(q):
    return q[0], q[1]
def packed(v, rng):
    q = [mx_ref.quantize(np.ascontiguousarray(v[r])) for r in range(N)]
    return np.stack([a for a, b in q]), np.stack([mx_ref.plane(b, rng) for a, b in q])
def values_of_codes():
    e, c = np.zeros((128, 128, 4), np.float32), np.zeros((128, 2, 4), np.uint8)
    e[np.arange(128), np.arange(128), 0] = 1
    c[:127, :, 0] = np.arange(256).reshape(2, 128).T[:127]
    return mx_ref.matmul(mx_ref.quantize(e.reshape(128, 512).astype(BF)), (c.reshape(128, 8), np.full((16, 2), 127, np.uint8))).T.reshape(-1).astype(np.float64)
CODE_VALUE, SCALE_VALUE = values_of_codes(), 2.0 ** (np.arange(256) - 127.0)
def decode(q):
    return (CODE_VALUE[q[0]].reshape(16, 8, -1, 4) * SCALE_VALUE[q[1]][:, None, :, None] + 0.0).reshape(128, -1).astype(np.float32)
def f(rng, *shape):
    return mx_ref.flush((rng.standard_normal(shape, dtype=np.float32) * np.exp2(rng.integers(-2, 3, shape[:-1] + (1,)))).astype(BF))
def wide(rng, *shape, cols=0):
    v = rng.standard_normal(shape, dtype=np.float32) * np.exp2(rng.integers(-12, 13, shape)).astype(np.float32)
    if cols: v *= np.repeat(np.exp2(rng.integers(-cols, cols + 1, shape[:-2] + (1, shape[-1] // 4))) * (rng.random(shape[:-2] + (1, shape[-1] // 4)) > 0.0625), 4, axis=-1).astype(np.float32)
    return mx_ref.flush(v.astype(BF))
C, STAGES = 288, 7
STEP = [4, 1, 2]
def numbers_of(rng):
    return {"x": np.array(f(rng, N, 128, 4 * C)), "u": np.array(f(rng, N, 128, 512)), "v": np.array(f(rng, N, 128, 512))}
def stored(a, b, s):
    return {"ta": np.stack([gtable(a[r]) for r in range(N)]), "tb": np.stack([gtable(b[r]) for r in range(N)]), "st": np.stack([gtable(s[r]) for r in range(N)])}
def lists(rng):
    e = np.tile(np.arange(C), (N, 8, 1))
    return stored(rng.permuted(e, axis=2), rng.permuted(e, axis=2), rng.permuted(e, axis=2))
def layers(rng):
    return np.array(f(rng, N, 128, 2048)).reshape(N, 8, 16, 4, 8, 16, 4)
def weights(rng, w):
    c, p = packed(np.ascontiguousarray(w).reshape(N, 128, 2048), rng)
    return {"wc": c, "ws": p}
def setup_inputs(rng):
    return {**numbers_of(rng), **lists(rng), **weights(rng, layers(rng))}
def setup_inputs_ties(rng):
    d = numbers_of(rng)
    o = rng.permutation(N)
    k = rng.integers(-1, 2, (2, N, 8, C)).astype(np.float32)
    k[0, o[1]] = 1
    x = d["x"].reshape(N, 8, 16, C, 4)
    x[:, :, [0, 1, 8]] = 0
    x[:, :, 0, :, 0] = k[0].astype(BF)
    x[:, :, 1, :, 0] = k[1].astype(BF)
    c = np.ones(N, np.float32)
    c[o[0]] = 0
    c[o[2]] = -1
    u = d["u"].reshape(N, 128, 128, 4)
    u[:, :, ::16] = 0
    for h in range(0, 128, 16):
        u[:, h, h, 0] = c.astype(BF)
        u[:, h + 8, h, 0] = c.astype(BF)
    w = layers(rng)
    w[:, :, :, :, :, [0, 1, 8]] = 0
    for g in range(8): w[:, g, 1, 0, g, 8, 0] = 32.0
    return {"x": x.reshape(N, 128, 4 * C), "u": u.reshape(N, 128, 512), "v": d["v"], **lists(rng), **weights(rng, w)}
def setup_inputs_near(rng):
    d = numbers_of(rng)
    o = rng.permutation(N) % 2
    k = np.where(o == 0, 2.0 ** -30, 1.0).astype(np.float32)
    x = np.zeros((N, 8, 16, C, 4), np.float32)
    s = rng.integers(-1, 2, (N, 8, C)) * k[:, None, None]
    x[:, :, 0, :, 0] = 1.125 * s
    x[:, :, 1, :, 0] = -1.25 * s
    for r in range(N):
        for g in rng.permutation(8)[:4]: x[r, g, 0, rng.integers(C), 0] = 2.0 ** 30 * rng.choice([-1.0, 1.0])
    x[:, :, 10, :, 0] = rng.integers(-1, 2, (N, 8, C)) * 2.0 ** -30
    x[:, :, 11, :, 0] = 2.0 ** -30
    u = d["u"].reshape(N, 128, 128, 4)
    u[:, :, ::16] = 0
    for h in range(0, 128, 16):
        u[:, h, h, 0] = (1.125 * k).astype(BF)
        u[:, h + 1, h, 0] = k.astype(BF)
        u[:, h + 8, h, 0] = k.astype(BF)
    w = np.zeros((N, 8, 16, 4, 8, 16, 4), np.float32)
    for g in range(8):
        w[:, g, 10, 0, g, 8, 0] = 2.0 ** -7
        w[:, g, 11, 0, g, 9, 0] = 2.0 ** 7
    for r in range(N):
        for g in rng.permutation(8)[:4]:
            w[r, g, 10, 0, g, 8, 0] = 2.0 ** -11
            w[r, g, 10, 0, g, 13, 0] = -2.0 ** -11
            w[r, g, 12, 0, g, 8, 0] = 2.0 ** -8
            w[r, g, 12, 0, g, 13, 0] = 2.0 ** -8
            w[r, g, 11, 0, g, 9, 0] = 2.0 ** 5
            u[r, 16 * g + 8, 16 * g, 0] = 1.125 * float(k[r])
            u[r, 16 * g + 13, 16 * g, 0] = float(k[r])
    return {"x": x.reshape(N, 128, 4 * C).astype(BF), "u": u.reshape(N, 128, 512), "v": d["v"], **lists(rng), **weights(rng, w.astype(BF))}
def setup_inputs_odd(rng):
    d = numbers_of(rng)
    x = (1.0 + (2 * rng.integers(0, 64, (N, 8, 16, C, 4)) + 1) * 2.0 ** -7) * np.exp2(-rng.integers(0, 7, (N, 8, 16, C, 4)).astype(np.float64)) * rng.choice([-1.0, 1.0], (N, 8, 16, C, 4))
    x[:, :, 0, :, 0] = 1.96875 * 2.0 ** 8 * rng.choice([-1.0, 1.0], (N, 8, C))
    x[:, :, 1:3] = 0
    x[:, :, 1, :, 0] = (8 + rng.integers(0, 2, (N, 8, C))) * 2.0 ** -8
    x[:, :, 2, :, 0] = -2.0 ** -5
    a = np.exp2(rng.integers(-3, 4, (N, 8, C)).astype(np.float64))
    x[:, :, 8:] = 0
    x[:, :, 8, :, 0] = 1.125 * a
    x[:, :, 11, :, 0] = (8 + rng.integers(0, 2, (N, 8, C))) * 2.0 ** -7 * a
    x[:, :, 12, :, 0] = 2.0 ** -4 * a
    u = d["u"].reshape(N, 128, 128, 4)
    u[:, :, ::16] = 0
    for h in range(0, 128, 16):
        for i in (1, 2, 9, 10): u[:, h + i, h, 0] = 1.0
    w = layers(rng)
    w[:, :, :3] = 0
    w[:, :, :, :, :, :3] = 0
    w[:, :, :, :, :, 8:] = 0
    for g in range(8):
        w[:, g, 8, 0, g, 8, 0] = 28.0
        w[:, g, 11, 0, g, 9, 0] = 2.0 ** -5
        w[:, g, 12, 0, g, 10, 0] = -2.0 ** -5
    return {"x": x.astype(np.float32).reshape(N, 128, 4 * C).astype(BF), "u": u.reshape(N, 128, 512), "v": d["v"], **lists(rng), **weights(rng, w)}
def setup_inputs_ends(rng):
    d = numbers_of(rng)
    o, e, h = rng.permutation(N) % 4, rng.permutation(N) % 4, rng.permutation(N) % 2
    s = rng.choice([-1.0, 1.0], (N, 8, 8, C, 4))
    s[o == 0] = -1
    s[o == 1] = rng.choice([-1.0, 1.0], (N, 1, 1, C, 1))[o == 1]
    low = s * (0.9 + 0.1 * rng.random((N, 8, 8, C, 4))) * 2.0 ** 30
    low[o == 3] = s[o == 3] * 2.0 ** -30
    x = d["x"].astype(np.float32).reshape(N, 8, 16, C, 4)
    x[:, :, :8] = low
    size = np.where(o == 3, 2.0 ** -30, 2.0 ** 30)
    c = np.stack([rng.permutation(8) % 2 * 2.0 - 1.0 for r in range(N)]) * size[:, None]
    u = d["u"].reshape(N, 128, 128, 4)
    u[:, :, ::16] = c.astype(np.float32).astype(BF)[:, None, :, None]
    v = rng.choice([-1.0, 1.0], (N, 128, 512)) * size[:, None, None]
    a, b, t = [rng.integers(0, C, (N, 8, C)) for i in range(3)]
    a[e == 0], b[e == 0], t[e == 0] = C - 1, C - 1, C - 1
    a[e == 1], b[e == 1], t[e == 1] = 0, C - 1, 0
    a[e == 2], b[e == 2], t[e == 2] = C - 1 - np.arange(C), np.arange(C), (np.arange(C) + 1) % 2 * (C - 1)
    w = np.zeros((N, 128, 4, 128, 4), np.float32)
    i = np.flatnonzero(np.arange(128) % 16 >= 8)
    for k in range(4): w[:, i, k, i, k] = np.where(h == 0, 2.0 ** 8, 2.0 ** -8)[:, None] * rng.choice([-1.0, 1.0], (N, 64))
    return {"x": x.reshape(N, 128, 4 * C).astype(BF), "u": u.reshape(N, 128, 512), "v": v.astype(np.float32).astype(BF), **stored(a, b, t), **weights(rng, w.astype(BF))}
def setup_inputs_spread(rng):
    d = setup_inputs(rng)
    d["x"] = wide(rng, N, 128, 4 * C, cols=6)
    return d
def check_inputs(d):
    b = []
    for k in ("x", "u", "v"):
        a = np.abs(d[k].astype(np.float32))
        if not (np.isfinite(a).all() and ((a == 0) | (a >= 2.0 ** -30) & (a <= 2.0 ** 30)).all()): b.append("a value of " + k)
    for k in ("ta", "tb", "st"):
        if not ((d[k] >= 0) & (d[k] < C)).all(): b.append("an entry of " + k)
    none, least, most = [emit(mx_ref.quantize(np.full((128, 16), k, np.float32).astype(BF)))[1][0, 0] for k in (0.0, 2.0 ** -8, 2.0 ** 8)]
    for r in range(N):
        if ((d["wc"][r] == 0x7F) | (d["wc"][r] == 0xFF)).any(): b.append("wc: a code that is no number")
        s = mx_ref.live(d["ws"][r])
        if ((s != none) & ((s < least) | (s > most))).any(): b.append("ws: a scale out of range")
    return b
def at(t, s):
    return np.take_along_axis(t, s, axis=2)
def reference(x, u, v, ta, tb, st, wc, ws):
    qu = [mx_ref.quantize(u[r]) for r in range(N)]
    lay = [pk(wc[r], ws[r]) for r in range(N)]
    a, b, s = [np.stack([gentries(k[r]) for r in range(N)]).astype(np.int64) for k in (ta, tb, st)]
    now = [x[r] for r in range(N)]
    for step in STEP:
        q = [mx_ref.quantize(now[r]) for r in range(N)]
        bit = np.stack([mx_ref.matmul(qu[r], q[r])[::16] > 0 for r in range(N)])
        for k in range(STAGES):
            right = np.roll(at(bit, s), -1, axis=2)
            s = np.where(right, at(b, s), at(a, s))
        z = [gcols(decode(q[r]).astype(BF), s[r]) for r in range(N)]
        qz = [mx_ref.quantize(z[r]) for r in range(N)]
        made, change = [], []
        for r in range(N):
            p = r ^ step
            h = tile([mx_ref.matmul(pick(lay[r], np.arange(128 * k, 128 * k + 128)), qz[p]) * np.float32(0.03125) for k in range(4)])
            change.append(mx_ref.matmul(qu[r], mx_ref.quantize(h))[::16] > 0)
            made.append((z[r].astype(np.float32) + gcols(h, s[p]).astype(np.float32)).astype(BF))
        c = np.stack(change)
        a, b = np.where(c, b, a), np.where(c, a, b)
        now = made
    y, op = np.zeros((N, 128, C), np.float32), np.zeros((N, 8, 3 * C), np.float32)
    oc, osc = np.zeros((N, 128, 4 * C), np.uint8), np.zeros((N, 16, C), np.uint8)
    for r in range(N):
        q = mx_ref.quantize(now[r])
        y[r] = mx_ref.matmul(mx_ref.quantize(v[r]), q)
        op[r] = np.concatenate([s[r], a[r], b[r]], axis=1)
        oc[r], osc[r] = emit(q)
    return {"y": y, "op": op, "oc": oc, "osc": osc}

@@ -1,0 +1,414 @@
+from concourse.bass import DstId, RemoteDMATransfer
+from concourse.mybir import dt, AluOpType, ActivationFunctionType
+
+STEP = [4, 1, 2]
+STAGES = 7
+C = 288
+HC = C // 2
+K = 336
+BIG = 2.0 ** 40
+TINY = -2.0 ** -100
+
+SCRATCH = {
+    "xin": ("sbuf", [128, 1152], "bfloat16"),
+    "ut": ("sbuf", [128, 512], "bfloat16"), "vt": ("sbuf", [128, 512], "bfloat16"),
+    "uq": ("sbuf", [128, 128], "float8_e4m3fn_x4"), "us": ("sbuf", [128, 128], "uint8"),
+    "ur": ("sbuf", [128, 128], "float8_e4m3fn_x4"), "urs": ("sbuf", [128, 128], "uint8"),
+    "vq": ("sbuf", [128, 128], "float8_e4m3fn_x4"), "vs": ("sbuf", [128, 128], "uint8"),
+    "wq": ("sbuf", [128, 512], "float8_e4m3fn_x4"), "wsc": ("sbuf", [128, 512], "uint8"),
+    "eb": ("sbuf", [128, 2048], "bfloat16"),
+    "eq": ("sbuf", [128, 512], "float8_e4m3fn_x4"), "es": ("sbuf", [128, 512], "uint8"),
+    "ei": ("sbuf", [128, 512], "bfloat16"),
+    "pi": ("sbuf", [128, 8], "int32"), "pk": ("sbuf", [128, 8], "int32"), "pf": ("sbuf", [128, 8], "float32"),
+    "sc16": ("sbuf", [128, 8], "float32"), "sc4": ("sbuf", [128, 8], "float32"), "tp": ("sbuf", [128, 8], "float32"),
+    "tm": ("sbuf", [128, 304], "bfloat16"), "tm4": ("sbuf", [128, 288], "bfloat16"),
+    "ma": ("sbuf", [128, 304], "bfloat16"), "mb": ("sbuf", [128, 304], "bfloat16"),
+    "mask16": ("sbuf", [128, 304], "bfloat16"), "mask4": ("sbuf", [128, 288], "bfloat16"),
+    "enc": ("sbuf", [128, 288], "bfloat16"), "idf": ("sbuf", [128, 288], "float32"),
+    "offui": ("sbuf", [128, 8], "int32"), "offu": ("sbuf", [128, 8], "uint16"),
+    "tai": ("sbuf", [128, 18], "int32"), "tbi": ("sbuf", [128, 18], "int32"), "sti": ("sbuf", [128, 18], "int32"),
+    "sl": ("sbuf", [128, 20], "uint16"), "lab": ("sbuf", [128, 36], "uint16"),
+    "ab": ("sbuf", [128, 36], "float32"), "dd": ("sbuf", [128, 36], "float32"), "m2": ("sbuf", [128, 36], "float32"),
+    "c01": ("sbuf", [128, 18], "float32"),
+    "sg": ("sbuf", [128, 288], "bfloat16"), "idsg": ("sbuf", [128, 288], "bfloat16"), "cs": ("sbuf", [128, 288], "bfloat16"),
+    "w": ("sbuf", [128, 688], "bfloat16"), "r": ("sbuf", [128, 320], "bfloat16"),
+    "so1": ("sbuf", [128, 304], "bfloat16"), "son": ("sbuf", [128, 304], "bfloat16"), "so4": ("sbuf", [128, 288], "bfloat16"),
+    "soc": ("sbuf", [128, 288], "bfloat16"),
+    "za": ("sbuf", [128, 20], "float32"), "tmp": ("sbuf", [128, 20], "float32"), "yy": ("sbuf", [128, 20], "float32"),
+    "off": ("sbuf", [128, 20], "uint16"),
+    "zs": ("sbuf", [128, 20], "float32"), "ts": ("sbuf", [128, 20], "float32"), "ys": ("sbuf", [128, 20], "float32"),
+    "z4": ("sbuf", [128, 72], "float32"), "t4": ("sbuf", [128, 72], "float32"), "y4": ("sbuf", [128, 72], "float32"),
+    "tt": ("sbuf", [128, 1152], "bfloat16"), "tq": ("sbuf", [128, 1152], "bfloat16"),
+    "zt": ("sbuf", [128, 1152], "bfloat16"), "zp": ("sbuf", [128, 1152], "bfloat16"), "h": ("sbuf", [128, 1152], "bfloat16"),
+    "zq": ("sbuf", [128, 288], "float8_e4m3fn_x4"), "zqs": ("sbuf", [128, 288], "uint8"),
+    "hq": ("sbuf", [128, 288], "float8_e4m3fn_x4"), "hqs": ("sbuf", [128, 288], "uint8"),
+    "opr": ("sbuf", [128, 864], "float32"), "yo": ("sbuf", [128, 288], "float32"),
+    "ps": ("psum", [128, 4096], "float32"),
+}
+for _r in range(4):
+    if _r:
+        SCRATCH["xt%d" % _r] = ("sbuf", [128, 1152], "bfloat16")
+    SCRATCH["qx%d" % _r] = ("sbuf", [128, 288], "float8_e4m3fn_x4")
+    SCRATCH["sx%d" % _r] = ("sbuf", [128, 288], "uint8")
+for _r in range(3):
+    SCRATCH["lq%d" % _r] = ("sbuf", [128, 288], "float8_e4m3fn_x4")
+    SCRATCH["lsx%d" % _r] = ("sbuf", [128, 288], "uint8")
+    SCRATCH["own%d" % _r] = ("sbuf", [128, 72], "uint16")
+    SCRATCH["arr%d" % _r] = ("sbuf", [128, 72], "uint16")
+
+DMAS = ["d%d" % _i for _i in range(20)]
+SEMAPHORES = ["cV", "cS", "cT", "cP", "left"] + ["ax%d" % _r for _r in range(3)] + ["al%d" % _r for _r in range(3)] + DMAS
+
+
+def make_tracker(g, T):
+    queues = {"V": g.vector, "S": g.scalar, "T": g.tensor, "P": g, "Y": g.sync}
+    csem = {"V": "cV", "S": "cS", "T": "cT", "P": "cP"}
+    count = {}
+    known = {q: {} for q in queues}
+    clocks = {}
+    writes, reads = {}, {}
+    ndma = [0]
+
+    def wait(q, toks):
+        todo = [t for t in set(toks) if known[q].get(t[0], 0) < t[1]]
+        best = {}
+        for s, v in todo:
+            best[s] = max(best.get(s, 0), v)
+        items = sorted(best.items())
+        for s, v in items:
+            if any(o[0] != s and clocks[o].get(s, 0) >= v for o in items):
+                continue
+            queues[q].wait_ge(T.sem[s], v)
+        for s, v in items:
+            for s2, v2 in clocks[(s, v)].items():
+                known[q][s2] = max(known[q].get(s2, 0), v2)
+            known[q][s] = max(known[q].get(s, 0), v)
+
+    def deps(q, rd, wr):
+        toks = []
+        for k, a, b in rd:
+            toks += [t for x, y, t, oq in writes.get(k, []) if x < b and a < y]
+        for k, a, b in wr:
+            toks += [t for x, y, t, oq in writes.get(k, []) if x < b and a < y]
+            toks += [t for x, y, t, oq in reads.get(k, []) if x < b and a < y and oq != q]
+        return toks
+
+    def note(q, rd, wr, tok):
+        for k, a, b in wr:
+            writes[k] = [e for e in writes.get(k, []) if not (a <= e[0] and e[1] <= b)] + [(a, b, tok, q)]
+            reads[k] = [e for e in reads.get(k, []) if not (a <= e[0] and e[1] <= b)]
+        for k, a, b in rd:
+            reads.setdefault(k, []).append((a, b, tok, q))
+
+    def op(q, call, rd, wr, dma=False):
+        wait(q, deps(q, rd, wr))
+        if dma:
+            s, inc = DMAS[ndma[0]], 16
+            ndma[0] += 1
+        else:
+            s, inc = csem[q], 1
+        count[s] = count.get(s, 0) + inc
+        tok = (s, count[s])
+        call(queues[q]).then_inc(T.sem[s], inc)
+        clocks[tok] = dict(known[q])
+        clocks[tok][s] = count[s]
+        note("dma" if dma else q, rd, wr, tok)
+
+    def arrival(s, v, wr):
+        clocks[(s, v)] = {s: v}
+        count[s] = v
+        note("net", [], wr, (s, v))
+
+    def before(q, rd):
+        wait(q, deps(q, rd, []))
+
+    def finish():
+        for s in sorted(count):
+            g.wait_ge(T.sem[s], count[s])
+
+    return op, arrival, before, finish, count
+
+
+def rank_program(g, core, T, topo):
+    rank = T.rank_of(core)
+    if rank is None:
+        return
+    A = AluOpType
+    F = ActivationFunctionType
+    op, arrival, before, finish, count = make_tracker(g, T)
+
+    def R(k, a=0, b=100000):
+        return (k, a, b)
+
+    def lanes(k, a=0, b=C):
+        return [(k + str(t), a, b) for t in range(4)]
+
+    def load(q, dst, src, key, a=0, b=100000):
+        op(q, lambda e: e.dma_start(dst, src), [], [(key, a, b)], dma=True)
+    load("Y", T.xin[:, 0:576], T.x[:, 0:576], "xin", 0, HC)
+    load("S", T.ut[:, :], T.u[:, :], "ut")
+    load("Y", T.xin[:, 576:1152], T.x[:, 576:1152], "xin", HC, C)
+    load("Y", T.sti[:, :], T.st[:, :], "sti")
+    load("S", T.tai[:, :], T.ta[:, :], "tai")
+    load("S", T.tbi[:, :], T.tb[:, :], "tbi")
+    load("Y", T.wq[:, :].bitcast(dt.uint8), T.wc[:, :], "wq")
+    load("Y", T.wsc[:, :], T.ws[:, :], "wsc")
+    load("Y", T.vt[:, :], T.v[:, :], "vt")
+
+    def V(call, rd, wr):
+        op("V", call, rd, wr)
+
+    def S(call, rd, wr):
+        op("S", call, rd, wr)
+
+    def P(out, pat, base, cm, key, flag=False):
+        if flag:
+            op("P", lambda e: e.iota(out, pat, base, cm, allow_small_or_imprecise_dtypes=True), [], [R(key)])
+        else:
+            op("P", lambda e: e.iota(out, pat, base, cm), [], [R(key)])
+    P(T.pi[:, 0:5], [[1, 5]], 0, 1, "pi")
+    P(T.offui[:, :], [[16, 8]], 0, 0, "offui")
+    P(T.tm[:, :], [[0, 19], [1, 16]], 0, 0, "tm", True)
+    op("P", lambda e: e.iota(T.enc[:, 0:256], [[1, 256]], 1, 0, allow_small_or_imprecise_dtypes=True), [], [R("enc", 0, 256)])
+    op("P", lambda e: e.iota(T.enc[:, 256:288], [[2, 32]], 258, 0, allow_small_or_imprecise_dtypes=True), [], [R("enc", 256, 288)])
+    P(T.ei[:, :], [[1, 512]], 0, -4, "ei", True)
+    P(T.tm4[:, :], [[0, 72], [1, 4]], 0, 0, "tm4", True)
+
+    V(lambda e: e.memset(T.r[:, 304:320], 1.0), [], [R("r", 304, 320)])
+    V(lambda e: e.memset(T.w[:, :], 1.0), [], [R("w", 0, 688)])
+    V(lambda e: e.tensor_copy(T.offu[:, :], T.offui[:, :]), [R("offui")], [R("offu")])
+    for j, (src, sh, an) in enumerate([(0, 0, 15), (1, 0, 15), (0, 2, 3), (4, 2, 3), (0, 0, 3)]):
+        if sh:
+            V(lambda e: e.tensor_scalar(T.pk[:, j:j + 1], T.pi[:, src:src + 1], sh, an, A.arith_shift_right, A.bitwise_and), [R("pi")], [R("pk", j, j + 1)])
+        else:
+            V(lambda e: e.tensor_scalar(T.pk[:, j:j + 1], T.pi[:, src:src + 1], an, None, A.bitwise_and), [R("pi")], [R("pk", j, j + 1)])
+    V(lambda e: e.tensor_copy(T.pf[:, 0:5], T.pk[:, 0:5]), [R("pk", 0, 5)], [R("pf")])
+    V(lambda e: e.tensor_scalar(T.sc16[:, 0:1], T.pf[:, 0:1], 15.0, 1.0 / BIG, A.is_equal, A.max), [R("pf")], [R("sc16")])
+    V(lambda e: e.tensor_scalar(T.ma[:, :], T.tm[:, :], T.pf[:, 1:2], BIG, A.is_equal, A.mult), [R("tm"), R("pf")], [R("ma")])
+    V(lambda e: e.tensor_scalar(T.mb[:, :], T.tm[:, :], T.pf[:, 0:1], None, A.not_equal), [R("tm"), R("pf")], [R("mb")])
+    V(lambda e: e.tensor_tensor(T.mask16[:, :], T.ma[:, :], T.mb[:, :], A.max), [R("ma"), R("mb")], [R("mask16")])
+    V(lambda e: e.quantize_mx(T.uq[:, :], T.us[:, :], T.ut[:, :]), [R("ut")], [R("uq")])
+    V(lambda e: e.tensor_copy(T.ur[:, 0:128].bitcast(dt.uint32), T.uq[:, 0:128].bitcast(dt.uint32).indirect(T.offu[:, 0:8])), [R("uq"), R("offu")], [R("ur")])
+    V(lambda e: e.tensor_copy(T.urs[:, 0:128], T.us[:, 0:128].indirect(T.offu[:, 0:8])), [R("uq"), R("offu")], [R("urs")])
+
+    def quant_x(r, hf, src):
+        a, b = hf * HC, hf * HC + HC
+        qc, qs, key = T["qx%d" % r], T["sx%d" % r], ("xin" if r == 0 else "xt%d" % r)
+        V(lambda e: e.quantize_mx(qc[:, a:b], qs[:, a:b], src[:, 4 * a:4 * b]), [R(key, a, b)], [R("qx%d" % r, a, b)])
+
+    def bank(i, n):
+        return T.ps[:, 512 * i:512 * i + n]
+
+    def mm(i, n, st, sts, stk, mv, mvs, mvk):
+        op("T", lambda e: e.matmul_mx(bank(i, n), st, sts, mv, mvs, True, True), stk + mvk, [R("B%d" % i)])
+
+    def score_half(r, hf):
+        a, b = hf * HC, hf * HC + HC
+        mm(hf, HC, T.ur[:, :], T.urs[:, :], [R("ur"), R("urs")], T["qx%d" % r][:, a:b], T["sx%d" % r][:, a:b], [R("qx%d" % r, a, b)])
+        S(lambda e: e.activation(T.sg[:, a:b], bank(hf, HC), F.Sign, bias=TINY), [R("B%d" % hf)], [R("sg", a, b)])
+
+    def idsg_half(hf):
+        a, b = hf * HC, hf * HC + HC
+        V(lambda e: e.tensor_tensor(T.idsg[:, a:b], T.sg[:, a:b], T.enc[:, a:b], A.mult), [R("sg", a, b), R("enc", a, b)], [R("idsg", a, b)])
+
+    def vgather(out, win, off, rd, wr):
+        V(lambda e: e.tensor_copy(out, win.indirect(off)), rd, wr)
+
+    def sgather(out, win, off, rd, wr):
+        S(lambda e: e.activation(out, win.indirect(off), F.Copy), rd, wr)
+
+    def scan(out, mask, row, rd, wr):
+        V(lambda e: e.tensor_tensor_scan(out, mask, row, 0.0, A.mult, A.add), rd, wr)
+
+    PARTS = {("A", 0): (0, 16, 1, 257, 1), ("A", 1): (16, 18, 258, 321, 2), ("B", 0): (18, 34, K + 1, K + 257, 1), ("B", 1): (34, 36, K + 258, K + 321, 2)}
+
+    def table(q, which, part):
+        a, b, c, d, st = PARTS[(which, part)]
+        fn = vgather if q == "V" else sgather
+        fn(T.w[:, c:d:st], T.idsg[:, 0:C], T.lab[:, a:b], [R("idsg"), R("lab", a, b)], [R("w", c, d)])
+
+    VC = 10
+
+    def stage_gather(t):
+        win, wk, off, ok = (T.idsg[:, 0:C], "idsg", T.sl, "sl") if t == 0 else (T.w[:, 0:672], "w", T.off, "off")
+        vgather(T.r[:, 0:16 * VC], win, off[:, 0:VC], [R(wk), R(ok)], [R("r", 0, 16 * VC)])
+        sgather(T.r[:, 16 * VC:304], win, off[:, VC:19], [R(wk), R(ok)], [R("r", 16 * VC, 304)])
+
+    def own_scan():
+        scan(T.so1[:, :], T.mask16[:, :], T.r[:, 0:304], [R("mask16"), R("r", 0, 304)], [R("so1")])
+
+    def list_abs(out, key):
+        S(lambda e: e.activation(out, T.so1[:, 15:304:16], F.Abs, scale=T.sc16[:, 0:1]), [R("so1"), R("sc16")], [R(key)])
+
+    def stage_list(fill):
+        own_scan()
+        scan(T.son[:, :], T.mask16[:, :], T.r[:, 1:305], [R("mask16"), R("r", 1, 305)], [R("son")])
+        fill()
+        list_abs(T.za[:, 0:19], "za")
+        V(lambda e: e.tensor_scalar(T.tmp[:, 0:19], T.son[:, 15:304:16], 0.0, float(K), A.is_gt, A.mult), [R("son")], [R("tmp")])
+        V(lambda e: e.tensor_tensor(T.yy[:, 0:19], T.za[:, 0:19], T.tmp[:, 0:19], A.add), [R("za"), R("tmp")], [R("yy")])
+        V(lambda e: e.tensor_copy(T.off[:, 0:19], T.yy[:, 0:19]), [R("yy")], [R("off")])
+
+    def unpack(qc, qs, keys, banks):
+        for b in range(4):
+            mm(banks[b], C, T.eq[:, 128 * b:128 * b + 128], T.es[:, 128 * b:128 * b + 128], [R("eq")], qc[:, :], qs[:, :], keys)
+
+    def pieces(buf, key, banks):
+        out = []
+        for b in range(4):
+            for hf in range(2):
+                a = hf * HC
+                out.append(lambda b=b, a=a: S(lambda e: e.activation(buf[:, 4 * a + b:4 * (a + HC):4], T.ps[:, 512 * banks[b] + a:512 * banks[b] + a + HC], F.Copy),
+                                              [R("B%d" % banks[b])], [(key + str(b), a, a + HC)]))
+        return out
+
+    V(lambda e: e.tensor_copy(T.sl[:, 0:18], T.sti[:, :]), [R("sti")], [R("sl", 0, 18)])
+    V(lambda e: e.tensor_copy(T.sl[:, 18:19], T.sti[:, 0:1]), [R("sti")], [R("sl", 18, 19)])
+    quant_x(0, 0, T.xin)
+    quant_x(0, 1, T.xin)
+    score_half(0, 0)
+    score_half(0, 1)
+    V(lambda e: e.tensor_copy(T.lab[:, 0:18], T.tai[:, :]), [R("tai")], [R("lab", 0, 18)])
+    V(lambda e: e.tensor_copy(T.lab[:, 18:36], T.tbi[:, :]), [R("tbi")], [R("lab", 18, 36)])
+    idsg_half(0)
+    idsg_half(1)
+
+    def more_constants():
+        V(lambda e: e.tensor_copy(T.ab[:, 0:18], T.tai[:, :]), [R("tai")], [R("ab", 0, 18)])
+        V(lambda e: e.tensor_copy(T.ab[:, 18:36], T.tbi[:, :]), [R("tbi")], [R("ab", 18, 36)])
+        V(lambda e: e.tensor_scalar(T.ma[:, 0:288], T.tm4[:, :], T.pf[:, 3:4], BIG, A.is_equal, A.mult), [R("tm4"), R("pf")], [R("ma")])
+        V(lambda e: e.tensor_scalar(T.mb[:, 0:288], T.tm4[:, :], T.pf[:, 2:3], None, A.not_equal), [R("tm4"), R("pf")], [R("mb")])
+        V(lambda e: e.tensor_tensor(T.mask4[:, :], T.ma[:, 0:288], T.mb[:, 0:288], A.max), [R("ma"), R("mb")], [R("mask4")])
+        V(lambda e: e.tensor_scalar(T.sc4[:, 1:2], T.pf[:, 2:3], 3.0, 1.0 / BIG, A.is_equal, A.max), [R("pf")], [R("sc4", 1, 2)])
+        V(lambda e: e.tensor_scalar(T.sc4[:, 0:1], T.sc4[:, 1:2], 4.0, None, A.mult), [R("sc4", 1, 2)], [R("sc4", 0, 1)])
+        V(lambda e: e.tensor_scalar(T.tp[:, 0:1], T.pf[:, 4:5], 508.0, None, A.add), [R("pf")], [R("tp")])
+
+    def unpackers():
+        for b in range(4):
+            V(lambda e: e.tensor_scalar(T.eb[:, 512 * b:512 * b + 512], T.ei[:, :], float(b), None, A.is_equal), [R("ei")], [R("eb", b, b + 1)])
+        V(lambda e: e.quantize_mx(T.eq[:, :], T.es[:, :], T.eb[:, :]), [R("eb", 0, 4)], [R("eq")])
+
+    def differences():
+        V(lambda e: e.tensor_tensor(T.dd[:, 0:18], T.ab[:, 18:36], T.ab[:, 0:18], A.subtract), [R("ab")], [R("dd", 0, 18)])
+        V(lambda e: e.tensor_tensor(T.dd[:, 18:36], T.ab[:, 0:18], T.ab[:, 18:36], A.subtract), [R("ab")], [R("dd", 18, 36)])
+
+    for r in range(3):
+        partner = T.cores[rank ^ STEP[r]]
+        rid, pid = topo.addr(partner, core)
+        engines = topo.engines(core, partner)[:8]
+        mask = sum(1 << e for e in engines)
+        ne = len(engines)
+        qc, qs = T["qx%d" % r], T["sx%d" % r]
+        lc, ls = T["lq%d" % r], T["lsx%d" % r]
+        own, arr = T["own%d" % r], T["arr%d" % r]
+
+        before("P", [R("qx%d" % r)])
+        g.remote_dma(lc[:, :].bitcast(dt.uint8), qc[:, :].bitcast(dt.uint8), T.sem["ax%d" % r], T.sem.left, pid, rid, mask)
+        g.remote_dma(ls[:, :], qs[:, :], T.sem["ax%d" % r], T.sem.left, pid, rid, mask)
+        count["left"] = count.get("left", 0) + 2 * ne
+        arrival("ax%d" % r, 2 * ne, [R("lq%d" % r)])
+        arrival("al%d" % r, ne, [R("arr%d" % r)])
+        if r == 0:
+            P(T.idf[:, :], [[1, 288]], 0, 0, "idf", True)
+
+        stage_gather(0)
+        stage_list(lambda: table("S", "A", 1))
+        table("S", "A", 0)
+        table("S", "B", 1)
+        table("V", "B", 0)
+        if r == 0:
+            unpackers()
+            more_constants()
+            differences()
+        unpack(qc, qs, [R("qx%d" % r)], [2, 3, 4, 5])
+        unpack(lc, ls, [R("lq%d" % r)], [6, 7, 0, 1])
+        todo = pieces(T.tt, "tt", [2, 3, 4, 5]) + pieces(T.tq, "tq", [6, 7, 0, 1])
+
+        for t in range(1, STAGES + 1):
+            stage_gather(t)
+            if t < STAGES:
+                stage_list(todo.pop(0))
+                todo.pop(0)()
+        scan(T.so4[:, :], T.mask4[:, :], T.r[:, 0:288], [R("mask4"), R("r", 0, 288)], [R("so4")])
+        S(lambda e: e.activation(T.z4[:, :], T.so4[:, 3:288:4], F.Abs, scale=T.sc4[:, 0:1]), [R("so4"), R("sc4", 0, 1)], [R("z4")])
+        V(lambda e: e.tensor_scalar(T.t4[:, :], T.z4[:, :], 1024.0, -0.5, A.max, A.mult), [R("z4")], [R("t4")])
+        V(lambda e: e.tensor_tensor(T.y4[:, :], T.z4[:, :], T.t4[:, :], A.add), [R("z4"), R("t4")], [R("y4")])
+        V(lambda e: e.tensor_scalar(own[:, :], T.y4[:, :], T.tp[:, 0:1], None, A.add), [R("y4"), R("tp")], [R("own%d" % r)])
+        before("P", [R("own%d" % r)])
+        g.remote_dma(arr[:, :], own[:, :], T.sem["al%d" % r], T.sem.left, pid, rid, mask)
+        count["left"] += ne
+        while todo:
+            todo.pop(0)()
+
+        ok = R("own%d" % r)
+        vgather(T.zt[:, 0:576], T.tt[:, 0:1152], own[:, 0:36], lanes("tt") + [ok], [R("zt", 0, HC)])
+        sgather(T.zt[:, 576:1152], T.tt[:, 0:1152], own[:, 36:72], lanes("tt") + [ok], [R("zt", HC, C)])
+        own_scan()
+        list_abs(T.zs[:, 0:19], "zs")
+        V(lambda e: e.tensor_scalar(T.ts[:, 0:18], T.zs[:, 0:18], 256.0, -0.5, A.max, A.mult), [R("zs")], [R("ts")])
+        V(lambda e: e.tensor_tensor(T.ys[:, 0:18], T.zs[:, 0:18], T.ts[:, 0:18], A.add), [R("zs"), R("ts")], [R("ys")])
+        V(lambda e: e.tensor_scalar(T.sl[:, 0:18], T.ys[:, 0:18], 127.0, None, A.add), [R("ys")], [R("sl", 0, 18)])
+        V(lambda e: e.tensor_scalar(T.sl[:, 18:19], T.ys[:, 0:1], 127.0, None, A.add), [R("ys")], [R("sl", 18, 19)])
+        if r == 0:
+            V(lambda e: e.quantize_mx(T.vq[:, :], T.vs[:, :], T.vt[:, :]), [R("vt")], [R("vq")])
+
+        ak = R("arr%d" % r)
+        vgather(T.zp[:, 0:576], T.tq[:, 0:1152], arr[:, 0:36], lanes("tq") + [ak], [R("zp", 0, HC)])
+        sgather(T.zp[:, 576:1152], T.tq[:, 0:1152], arr[:, 36:72], lanes("tq") + [ak], [R("zp", HC, C)])
+        for hf in range(2):
+            a, b = hf * HC, hf * HC + HC
+            V(lambda e: e.quantize_mx(T.zq[:, a:b], T.zqs[:, a:b], T.zp[:, 4 * a:4 * b]), [R("zp", a, b)], [R("zq", a, b)])
+            for k in (0, 2, 1, 3):
+                mm(4 * hf + k, HC, T.wq[:, 128 * k:128 * k + 128], T.wsc[:, 128 * k:128 * k + 128], [R("wq"), R("wsc")], T.zq[:, a:b], T.zqs[:, a:b], [R("zq", a, b)])
+        for hf in range(2):
+            a, b = hf * HC, hf * HC + HC
+            for k in (0, 2, 1, 3):
+                i = 4 * hf + k
+                out = T.h[:, 4 * a + k:4 * b:4]
+                if k < 2:
+                    V(lambda e: e.tensor_scalar(out, bank(i, HC), 0.03125, None, A.mult), [R("B%d" % i)], [("h%d" % k, a, b)])
+                else:
+                    S(lambda e: e.activation(out, bank(i, HC), F.Copy, scale=0.03125), [R("B%d" % i)], [("h%d" % k, a, b)])
+
+        V(lambda e: e.quantize_mx(T.hq[:, :], T.hqs[:, :], T.h[:, :]), lanes("h"), [R("hq")])
+        mm(2, C, T.ur[:, :], T.urs[:, :], [R("ur"), R("urs")], T.hq[:, :], T.hqs[:, :], [R("hq")])
+        S(lambda e: e.activation(T.cs[:, :], bank(2, C), F.Sign, bias=TINY), [R("B2")], [R("cs")])
+        xt, xk = T["xt%d" % (r + 1)], "xt%d" % (r + 1)
+
+        def new_half(hf):
+            a, b = hf * HC, hf * HC + HC
+            V(lambda e: e.tensor_tensor(xt[:, 4 * a:4 * b], T.h[:, 0:1152].indirect(arr[:, 36 * hf:36 * hf + 36]), T.zt[:, 4 * a:4 * b], A.add),
+              lanes("h") + [ak, R("zt", a, b)], [R(xk, a, b)])
+        new_half(0)
+        quant_x(r + 1, 0, xt)
+        scan(T.soc[:, :], T.mask16[:, 0:288], T.cs[:, :], [R("mask16"), R("cs")], [R("soc")])
+        V(lambda e: e.tensor_scalar(T.c01[:, :], T.soc[:, 15:288:16], 0.0, None, A.is_gt), [R("soc")], [R("c01")])
+        V(lambda e: e.tensor_tensor(T.m2[:, 0:18], T.dd[:, 0:18], T.c01[:, :], A.mult), [R("dd", 0, 18), R("c01")], [R("m2", 0, 18)])
+        V(lambda e: e.tensor_tensor(T.m2[:, 18:36], T.dd[:, 18:36], T.c01[:, :], A.mult), [R("dd", 18, 36), R("c01")], [R("m2", 18, 36)])
+        V(lambda e: e.tensor_tensor(T.ab[:, :], T.ab[:, :], T.m2[:, :], A.add), [R("ab"), R("m2", 0, 36)], [R("ab")])
+        V(lambda e: e.tensor_copy(T.lab[:, :], T.ab[:, :]), [R("ab")], [R("lab", 0, 36)])
+        if r < 2:
+            score_half(r + 1, 0)
+        else:
+            for i in range(3):
+                lo, lk = (T.sl[:, 0:18], "sl") if i == 0 else (T.lab[:, 18 * i - 18:18 * i], "lab")
+                sgather(T.opr[:, C * i:C * i + C], T.idf[:, 0:C], lo, [R("idf"), R(lk)], [R("opr", i, i + 1)])
+            op("Y", lambda e: e.dma_start(T.op[:, :], T.opr[0:128:16, :]), [R("opr", 0, 3)], [], dma=True)
+        new_half(1)
+        quant_x(r + 1, 1, xt)
+        if r < 2:
+            score_half(r + 1, 1)
+            idsg_half(0)
+            idsg_half(1)
+            differences()
+
+    for hf in range(2):
+        a, b = hf * HC, hf * HC + HC
+        mm(3 + hf, HC, T.vq[:, :], T.vs[:, :], [R("vq")], T.qx3[:, a:b], T.sx3[:, a:b], [R("qx3", a, b)])
+    V(lambda e: e.tensor_copy(T.yo[:, 0:HC], bank(3, HC)), [R("B3")], [R("yo", 0, HC)])
+    op("Y", lambda e: e.dma_start(T.oc[:, :], T.qx3[:, :].bitcast(dt.uint8)), [R("qx3")], [], dma=True)
+    for k in range(4):
+        op("Y", lambda e: e.dma_start(T.osc[4 * k:4 * k + 4, :], T.sx3[32 * k:32 * k + 4, :]), [R("qx3")], [], dma=True)
+    S(lambda e: e.activation(T.yo[:, HC:C], bank(4, HC), F.Copy), [R("B4")], [R("yo", HC, C)])
+    op("S", lambda e: e.dma_start(T.y[:, :], T.yo[:, :]), [R("yo")], [], dma=True)
+    finish()

@@ -5,56 +5,30 @@ STEP = [4, 1, 2]
 STAGES = 7
 C = 288
 HC = C // 2
-K = 336
+MID = 336
+K = 672
 BIG = 2.0 ** 40
+UP = 2.0 ** 36
 TINY = -2.0 ** -100
 
-SCRATCH = {
-    "xin": ("sbuf", [128, 1152], "bfloat16"),
-    "ut": ("sbuf", [128, 512], "bfloat16"), "vt": ("sbuf", [128, 512], "bfloat16"),
-    "uq": ("sbuf", [128, 128], "float8_e4m3fn_x4"), "us": ("sbuf", [128, 128], "uint8"),
-    "ur": ("sbuf", [128, 128], "float8_e4m3fn_x4"), "urs": ("sbuf", [128, 128], "uint8"),
-    "vq": ("sbuf", [128, 128], "float8_e4m3fn_x4"), "vs": ("sbuf", [128, 128], "uint8"),
-    "wq": ("sbuf", [128, 512], "float8_e4m3fn_x4"), "wsc": ("sbuf", [128, 512], "uint8"),
-    "eb": ("sbuf", [128, 2048], "bfloat16"),
-    "eq": ("sbuf", [128, 512], "float8_e4m3fn_x4"), "es": ("sbuf", [128, 512], "uint8"),
-    "ei": ("sbuf", [128, 512], "bfloat16"),
-    "pi": ("sbuf", [128, 8], "int32"), "pk": ("sbuf", [128, 8], "int32"), "pf": ("sbuf", [128, 8], "float32"),
-    "sc16": ("sbuf", [128, 8], "float32"), "sc4": ("sbuf", [128, 8], "float32"), "tp": ("sbuf", [128, 8], "float32"),
-    "tm": ("sbuf", [128, 304], "bfloat16"), "tm4": ("sbuf", [128, 288], "bfloat16"),
-    "ma": ("sbuf", [128, 304], "bfloat16"), "mb": ("sbuf", [128, 304], "bfloat16"),
-    "mask16": ("sbuf", [128, 304], "bfloat16"), "mask4": ("sbuf", [128, 288], "bfloat16"),
-    "enc": ("sbuf", [128, 288], "bfloat16"), "idf": ("sbuf", [128, 288], "float32"),
-    "offui": ("sbuf", [128, 8], "int32"), "offu": ("sbuf", [128, 8], "uint16"),
-    "tai": ("sbuf", [128, 18], "int32"), "tbi": ("sbuf", [128, 18], "int32"), "sti": ("sbuf", [128, 18], "int32"),
-    "sl": ("sbuf", [128, 20], "uint16"), "lab": ("sbuf", [128, 36], "uint16"),
-    "ab": ("sbuf", [128, 36], "float32"), "dd": ("sbuf", [128, 36], "float32"), "m2": ("sbuf", [128, 36], "float32"),
-    "c01": ("sbuf", [128, 18], "float32"),
-    "sg": ("sbuf", [128, 288], "bfloat16"), "idsg": ("sbuf", [128, 288], "bfloat16"), "cs": ("sbuf", [128, 288], "bfloat16"),
-    "w": ("sbuf", [128, 688], "bfloat16"), "r": ("sbuf", [128, 320], "bfloat16"),
-    "so1": ("sbuf", [128, 304], "bfloat16"), "son": ("sbuf", [128, 304], "bfloat16"), "so4": ("sbuf", [128, 288], "bfloat16"),
-    "soc": ("sbuf", [128, 288], "bfloat16"),
-    "za": ("sbuf", [128, 20], "float32"), "tmp": ("sbuf", [128, 20], "float32"), "yy": ("sbuf", [128, 20], "float32"),
-    "off": ("sbuf", [128, 20], "uint16"),
-    "zs": ("sbuf", [128, 20], "float32"), "ts": ("sbuf", [128, 20], "float32"), "ys": ("sbuf", [128, 20], "float32"),
-    "z4": ("sbuf", [128, 72], "float32"), "t4": ("sbuf", [128, 72], "float32"), "y4": ("sbuf", [128, 72], "float32"),
-    "tt": ("sbuf", [128, 1152], "bfloat16"), "tq": ("sbuf", [128, 1152], "bfloat16"),
-    "zt": ("sbuf", [128, 1152], "bfloat16"), "zp": ("sbuf", [128, 1152], "bfloat16"), "h": ("sbuf", [128, 1152], "bfloat16"),
-    "zq": ("sbuf", [128, 288], "float8_e4m3fn_x4"), "zqs": ("sbuf", [128, 288], "uint8"),
-    "hq": ("sbuf", [128, 288], "float8_e4m3fn_x4"), "hqs": ("sbuf", [128, 288], "uint8"),
-    "opr": ("sbuf", [128, 864], "float32"), "yo": ("sbuf", [128, 288], "float32"),
-    "ps": ("psum", [128, 4096], "float32"),
-}
-for _r in range(4):
-    if _r:
-        SCRATCH["xt%d" % _r] = ("sbuf", [128, 1152], "bfloat16")
-    SCRATCH["qx%d" % _r] = ("sbuf", [128, 288], "float8_e4m3fn_x4")
-    SCRATCH["sx%d" % _r] = ("sbuf", [128, 288], "uint8")
-for _r in range(3):
-    SCRATCH["lq%d" % _r] = ("sbuf", [128, 288], "float8_e4m3fn_x4")
-    SCRATCH["lsx%d" % _r] = ("sbuf", [128, 288], "uint8")
-    SCRATCH["own%d" % _r] = ("sbuf", [128, 72], "uint16")
-    SCRATCH["arr%d" % _r] = ("sbuf", [128, 72], "uint16")
+SCRATCH = {"ps": ("psum", [128, 4096], "float32")}
+
+
+def _bufs(where, dtype, **cols):
+    for k in cols:
+        SCRATCH[k] = (where, [128, cols[k]], dtype)
+
+
+_bufs("sbuf", "bfloat16", xin=1152, xt1=1152, xt2=1152, xt3=1152, ut=512, vt=512, ones=512, eb=2048, tm=304, tm4=288, ma=304, mb=304,
+      mask16=304, mask4=288, enc=288, sg=288, idsg=288, cs=288, w=1344, r=320, so1=304, son=304, soc=288,
+      tt=1152, tq=1152, zt=1152, zp=1152, h=1152)
+for _n, _c in [("u", 128), ("ur", 128), ("v", 128), ("w", 512), ("e", 512), ("z", 288), ("h", 288)] + [("x%d" % _r, 288) for _r in range(4)] + [("l%d" % _r, 288) for _r in range(3)]:
+    SCRATCH["q" + _n] = ("sbuf", [128, _c], "float8_e4m3fn_x4")
+    SCRATCH["p" + _n] = ("sbuf", [128, _c], "uint8")
+_bufs("sbuf", "int32", pi=8, pk=8, offui=8, tai=18, tbi=18, sti=18)
+_bufs("sbuf", "float32", pf=8, sc16=8, kp=8, sc4=8, tp=8, revf=20, idf=288, ab=36, dd=36, m2=36, c01=18, za=20, tmp=20, yy=20,
+      wl=1344, rl=304, so4=288, sol=304, opr=864, yo=288)
+_bufs("sbuf", "uint16", offu=8, rev=20, sl=20, lab=36, off=20, own0=72, own1=72, own2=72, arr0=72, arr1=72, arr2=72)
 
 DMAS = ["d%d" % _i for _i in range(20)]
 SEMAPHORES = ["cV", "cS", "cT", "cP", "left"] + ["ax%d" % _r for _r in range(3)] + ["al%d" % _r for _r in range(3)] + DMAS
@@ -70,15 +44,14 @@ def make_tracker(g, T):
     ndma = [0]
 
     def wait(q, toks):
-        todo = [t for t in set(toks) if known[q].get(t[0], 0) < t[1]]
         best = {}
-        for s, v in todo:
-            best[s] = max(best.get(s, 0), v)
+        for s, v in toks:
+            if known[q].get(s, 0) < v:
+                best[s] = max(best.get(s, 0), v)
         items = sorted(best.items())
         for s, v in items:
-            if any(o[0] != s and clocks[o].get(s, 0) >= v for o in items):
-                continue
-            queues[q].wait_ge(T.sem[s], v)
+            if not any(o[0] != s and clocks[o].get(s, 0) >= v for o in items):
+                queues[q].wait_ge(T.sem[s], v)
         for s, v in items:
             for s2, v2 in clocks[(s, v)].items():
                 known[q][s2] = max(known[q].get(s2, 0), v2)
@@ -86,11 +59,10 @@ def make_tracker(g, T):
 
     def deps(q, rd, wr):
         toks = []
-        for k, a, b in rd:
+        for k, a, b in rd + wr:
             toks += [t for x, y, t, oq in writes.get(k, []) if x < b and a < y]
         for k, a, b in wr:
-            toks += [t for x, y, t, oq in writes.get(k, []) if x < b and a < y]
-            toks += [t for x, y, t, oq in reads.get(k, []) if x < b and a < y and oq != q]
+            toks += [t for x, y, t, oq in reads.get(k, []) if x < b and a < y and (oq != q or k in ("w", "wl"))]
         return toks
 
     def note(q, rd, wr, tok):
@@ -102,11 +74,10 @@ def make_tracker(g, T):
 
     def op(q, call, rd, wr, dma=False):
         wait(q, deps(q, rd, wr))
+        s, inc = csem.get(q), 1
         if dma:
             s, inc = DMAS[ndma[0]], 16
             ndma[0] += 1
-        else:
-            s, inc = csem[q], 1
         count[s] = count.get(s, 0) + inc
         tok = (s, count[s])
         call(queues[q]).then_inc(T.sem[s], inc)
@@ -141,7 +112,49 @@ def rank_program(g, core, T, topo):
         return (k, a, b)
 
     def lanes(k, a=0, b=C):
-        return [(k + str(t), a, b) for t in range(4)]
+        return [(k + "_" + str(t), a, b) for t in range(4)]
+
+    def V(call, rd, wr):
+        op("V", call, rd, wr)
+
+    def S(call, rd, wr):
+        op("S", call, rd, wr)
+
+    def ap(x):
+        if not isinstance(x, tuple):
+            return x
+        return T[x[0]][:, x[1]:x[2]:x[3]] if len(x) > 3 else T[x[0]][:, x[1]:x[2]]
+
+    def rgs(*xs):
+        return [(x[0], x[1], x[2]) for x in xs if isinstance(x, tuple)]
+
+    def ts(out, in0, s1, s2, *ops):
+        V(lambda e: e.tensor_scalar(ap(out), ap(in0), ap(s1), ap(s2), *ops), rgs(in0, s1, s2), rgs(out))
+
+    def tt(out, in0, in1, o):
+        V(lambda e: e.tensor_tensor(ap(out), ap(in0), ap(in1), o), rgs(in0, in1), rgs(out))
+
+    def cp(out, in_):
+        V(lambda e: e.tensor_copy(ap(out), ap(in_)), rgs(in_), rgs(out))
+
+    def act(out, in_, fn, **k):
+        S(lambda e: e.activation(ap(out), ap(in_), fn, **{x: ap(k[x]) for x in k}), rgs(in_, *k.values()), rgs(out))
+
+    def gather(q, out, win, off, wr=None, rd=None):
+        rr, ww = rgs(off) + (rd if rd else rgs(win)), wr if wr else rgs(out)
+        if q == "V":
+            V(lambda e: e.tensor_copy(ap(out), ap(win).indirect(ap(off))), rr, ww)
+        else:
+            S(lambda e: e.activation(ap(out), ap(win).indirect(ap(off)), F.Copy), rr, ww)
+
+    def iota(out, pat, base, cm, flag=True):
+        if flag:
+            op("P", lambda e: e.iota(ap(out), pat, base, cm, allow_small_or_imprecise_dtypes=True), [], rgs(out))
+        else:
+            op("P", lambda e: e.iota(ap(out), pat, base, cm), [], rgs(out))
+
+    def quant(q, a, b, src, rd):
+        V(lambda e: e.quantize_mx(T["q" + q][:, a:b], T["p" + q][:, a:b], T[src][:, 4 * a:4 * b]), rd, [R("q" + q, a, b)])
 
     def load(q, dst, src, key, a=0, b=100000):
         op(q, lambda e: e.dma_start(dst, src), [], [(key, a, b)], dma=True)
@@ -151,146 +164,162 @@ def rank_program(g, core, T, topo):
     load("Y", T.sti[:, :], T.st[:, :], "sti")
     load("S", T.tai[:, :], T.ta[:, :], "tai")
     load("S", T.tbi[:, :], T.tb[:, :], "tbi")
-    load("Y", T.wq[:, :].bitcast(dt.uint8), T.wc[:, :], "wq")
-    load("Y", T.wsc[:, :], T.ws[:, :], "wsc")
+    load("Y", T.qw[:, :].bitcast(dt.uint8), T.wc[:, :], "qw")
+    load("Y", T.pw[:, :], T.ws[:, :], "pw")
     load("Y", T.vt[:, :], T.v[:, :], "vt")
 
-    def V(call, rd, wr):
-        op("V", call, rd, wr)
+    def unpacker(b):
+        op("P", lambda e: e.affine_select(T.eb[:, 512 * b:512 * b + 512], T.ones[:, :], [[1, 512]], A.is_equal, 0.0, -b, -4), [R("ones", 0, 512)], [R("eb", b, b + 1)])
 
-    def S(call, rd, wr):
-        op("S", call, rd, wr)
+    iota(("pi", 0, 5), [[1, 5]], 0, 1, False)
+    iota(("offui", 0, 8), [[16, 8]], 0, 0, False)
+    iota(("tm", 0, 304), [[0, 19], [1, 16]], 0, 0)
+    iota(("enc", 0, 256), [[1, 256]], 1, 0)
+    iota(("enc", 256, 288), [[2, 32]], 258, 0)
+    iota(("revf", 0, 20), [[-16, 20]], 320, 0)
+    iota(("tm4", 0, 288), [[0, 72], [1, 4]], 0, 0)
 
-    def P(out, pat, base, cm, key, flag=False):
-        if flag:
-            op("P", lambda e: e.iota(out, pat, base, cm, allow_small_or_imprecise_dtypes=True), [], [R(key)])
-        else:
-            op("P", lambda e: e.iota(out, pat, base, cm), [], [R(key)])
-    P(T.pi[:, 0:5], [[1, 5]], 0, 1, "pi")
-    P(T.offui[:, :], [[16, 8]], 0, 0, "offui")
-    P(T.tm[:, :], [[0, 19], [1, 16]], 0, 0, "tm", True)
-    op("P", lambda e: e.iota(T.enc[:, 0:256], [[1, 256]], 1, 0, allow_small_or_imprecise_dtypes=True), [], [R("enc", 0, 256)])
-    op("P", lambda e: e.iota(T.enc[:, 256:288], [[2, 32]], 258, 0, allow_small_or_imprecise_dtypes=True), [], [R("enc", 256, 288)])
-    P(T.ei[:, :], [[1, 512]], 0, -4, "ei", True)
-    P(T.tm4[:, :], [[0, 72], [1, 4]], 0, 0, "tm4", True)
-
+    V(lambda e: e.memset(T.ones[:, :], 1.0), [], [R("ones", 0, 512)])
     V(lambda e: e.memset(T.r[:, 304:320], 1.0), [], [R("r", 304, 320)])
-    V(lambda e: e.memset(T.w[:, :], 1.0), [], [R("w", 0, 688)])
-    V(lambda e: e.tensor_copy(T.offu[:, :], T.offui[:, :]), [R("offui")], [R("offu")])
-    for j, (src, sh, an) in enumerate([(0, 0, 15), (1, 0, 15), (0, 2, 3), (4, 2, 3), (0, 0, 3)]):
+    for win in ("w", "wl"):
+        for a in (0, 512, 1024):
+            b = min(a + 512, 1344)
+            act((win, a, b), ("ones", 0, b - a), F.Copy)
+    unpacker(0)
+    unpacker(1)
+    for j, (src, sh, an) in enumerate([(0, 0, 15), (1, 0, 15), (0, 2, 3), (0, 0, 3)]):
         if sh:
-            V(lambda e: e.tensor_scalar(T.pk[:, j:j + 1], T.pi[:, src:src + 1], sh, an, A.arith_shift_right, A.bitwise_and), [R("pi")], [R("pk", j, j + 1)])
+            ts(("pk", j, j + 1), ("pi", src, src + 1), sh, an, A.arith_shift_right, A.bitwise_and)
         else:
-            V(lambda e: e.tensor_scalar(T.pk[:, j:j + 1], T.pi[:, src:src + 1], an, None, A.bitwise_and), [R("pi")], [R("pk", j, j + 1)])
-    V(lambda e: e.tensor_copy(T.pf[:, 0:5], T.pk[:, 0:5]), [R("pk", 0, 5)], [R("pf")])
-    V(lambda e: e.tensor_scalar(T.sc16[:, 0:1], T.pf[:, 0:1], 15.0, 1.0 / BIG, A.is_equal, A.max), [R("pf")], [R("sc16")])
-    V(lambda e: e.tensor_scalar(T.ma[:, :], T.tm[:, :], T.pf[:, 1:2], BIG, A.is_equal, A.mult), [R("tm"), R("pf")], [R("ma")])
-    V(lambda e: e.tensor_scalar(T.mb[:, :], T.tm[:, :], T.pf[:, 0:1], None, A.not_equal), [R("tm"), R("pf")], [R("mb")])
-    V(lambda e: e.tensor_tensor(T.mask16[:, :], T.ma[:, :], T.mb[:, :], A.max), [R("ma"), R("mb")], [R("mask16")])
-    V(lambda e: e.quantize_mx(T.uq[:, :], T.us[:, :], T.ut[:, :]), [R("ut")], [R("uq")])
-    V(lambda e: e.tensor_copy(T.ur[:, 0:128].bitcast(dt.uint32), T.uq[:, 0:128].bitcast(dt.uint32).indirect(T.offu[:, 0:8])), [R("uq"), R("offu")], [R("ur")])
-    V(lambda e: e.tensor_copy(T.urs[:, 0:128], T.us[:, 0:128].indirect(T.offu[:, 0:8])), [R("uq"), R("offu")], [R("urs")])
+            ts(("pk", j, j + 1), ("pi", src, src + 1), an, None, A.bitwise_and)
+    cp(("offu", 0, 8), ("offui", 0, 8))
+    cp(("pf", 0, 4), ("pk", 0, 4))
+    p16, q16, p4, t4 = [("pf", j, j + 1) for j in range(4)]
+    ts(("ma", 0, 304), ("tm", 0, 304), q16, BIG, A.is_equal, A.mult)
+    ts(("mb", 0, 304), ("tm", 0, 304), p16, None, A.not_equal)
+    ts(("sc16", 0, 1), p16, 15.0, 1.0 / BIG, A.is_equal, A.max)
+    tt(("mask16", 0, 304), ("ma", 0, 304), ("mb", 0, 304), A.max)
+    quant("u", 0, 128, "ut", [R("ut")])
+    V(lambda e: e.tensor_copy(T.qur[:, 0:128].bitcast(dt.uint32), T.qu[:, 0:128].bitcast(dt.uint32).indirect(T.offu[:, 0:8])), [R("qu"), R("offu")], [R("qur", 0, 1)])
+    V(lambda e: e.tensor_copy(T.pur[:, 0:128], T.pu[:, 0:128].indirect(T.offu[:, 0:8])), [R("qu"), R("offu")], [R("qur", 1, 2)])
 
-    def quant_x(r, hf, src):
-        a, b = hf * HC, hf * HC + HC
-        qc, qs, key = T["qx%d" % r], T["sx%d" % r], ("xin" if r == 0 else "xt%d" % r)
-        V(lambda e: e.quantize_mx(qc[:, a:b], qs[:, a:b], src[:, 4 * a:4 * b]), [R(key, a, b)], [R("qx%d" % r, a, b)])
+    def quant_x(r, hf):
+        src = "xt%d" % r if r else "xin"
+        quant("x%d" % r, hf * HC, hf * HC + HC, src, [R(src, hf * HC, hf * HC + HC)])
 
     def bank(i, n):
         return T.ps[:, 512 * i:512 * i + n]
 
-    def mm(i, n, st, sts, stk, mv, mvs, mvk):
-        op("T", lambda e: e.matmul_mx(bank(i, n), st, sts, mv, mvs, True, True), stk + mvk, [R("B%d" % i)])
+    def mm(i, st, sa, stk, mv, a, b):
+        op("T", lambda e: e.matmul_mx(bank(i, b - a), T["q" + st][:, sa:sa + 128], T["p" + st][:, sa:sa + 128], T["q" + mv][:, a:b], T["p" + mv][:, a:b], True, True),
+           stk + [R("q" + mv, a, b)], [R("B%d" % i)])
+
+    ukeys = [R("qur", 0, 2)]
 
     def score_half(r, hf):
         a, b = hf * HC, hf * HC + HC
-        mm(hf, HC, T.ur[:, :], T.urs[:, :], [R("ur"), R("urs")], T["qx%d" % r][:, a:b], T["sx%d" % r][:, a:b], [R("qx%d" % r, a, b)])
+        mm(hf, "ur", 0, ukeys, "x%d" % r, a, b)
         S(lambda e: e.activation(T.sg[:, a:b], bank(hf, HC), F.Sign, bias=TINY), [R("B%d" % hf)], [R("sg", a, b)])
 
     def idsg_half(hf):
         a, b = hf * HC, hf * HC + HC
-        V(lambda e: e.tensor_tensor(T.idsg[:, a:b], T.sg[:, a:b], T.enc[:, a:b], A.mult), [R("sg", a, b), R("enc", a, b)], [R("idsg", a, b)])
+        tt(("idsg", a, b), ("sg", a, b), ("enc", a, b), A.mult)
 
-    def vgather(out, win, off, rd, wr):
-        V(lambda e: e.tensor_copy(out, win.indirect(off)), rd, wr)
+    def scan(out, mask, row):
+        V(lambda e: e.tensor_tensor_scan(ap(out), ap(mask), ap(row), 0.0, A.mult, A.add), rgs(mask, row), rgs(out))
 
-    def sgather(out, win, off, rd, wr):
-        S(lambda e: e.activation(out, win.indirect(off), F.Copy), rd, wr)
+    def table(q, dst, src, first, tail):
+        m, c = (MID, 0) if first else (MID + K, 18)
+        if tail:
+            gather(q, (dst, m + 258, m + 321, 2), (src, 0, C), ("lab", c + 16, c + 18))
+        else:
+            gather(q, (dst, m + 1, m + 257), (src, 0, C), ("lab", c, c + 16))
 
-    def scan(out, mask, row, rd, wr):
-        V(lambda e: e.tensor_tensor_scan(out, mask, row, 0.0, A.mult, A.add), rd, wr)
-
-    PARTS = {("A", 0): (0, 16, 1, 257, 1), ("A", 1): (16, 18, 258, 321, 2), ("B", 0): (18, 34, K + 1, K + 257, 1), ("B", 1): (34, 36, K + 258, K + 321, 2)}
-
-    def table(q, which, part):
-        a, b, c, d, st = PARTS[(which, part)]
-        fn = vgather if q == "V" else sgather
-        fn(T.w[:, c:d:st], T.idsg[:, 0:C], T.lab[:, a:b], [R("idsg"), R("lab", a, b)], [R("w", c, d)])
+    def mirror(first):
+        m = MID if first else MID + K
+        gather("S", ("w", m - 320, m), ("w", m, m + 336), ("rev", 0, 20))
 
     VC = 10
 
     def stage_gather(t):
-        win, wk, off, ok = (T.idsg[:, 0:C], "idsg", T.sl, "sl") if t == 0 else (T.w[:, 0:672], "w", T.off, "off")
-        vgather(T.r[:, 0:16 * VC], win, off[:, 0:VC], [R(wk), R(ok)], [R("r", 0, 16 * VC)])
-        sgather(T.r[:, 16 * VC:304], win, off[:, VC:19], [R(wk), R(ok)], [R("r", 16 * VC, 304)])
+        row, win, off = "r", ("w", 0, 2 * K), "off"
+        if t == 0:
+            win, off = ("idsg", 0, C), "sl"
+        elif t == STAGES:
+            row, win = "rl", ("wl", 0, 2 * K)
+        gather("V", (row, 0, 16 * VC), win, (off, 0, VC))
+        gather("S", (row, 16 * VC, 304), win, (off, VC, 19))
+
+    M16, M4, SC16, SC4 = ("mask16", 0, 304), ("mask4", 0, 288), ("sc16", 0, 1), ("sc4", 4, 5)
 
     def own_scan():
-        scan(T.so1[:, :], T.mask16[:, :], T.r[:, 0:304], [R("mask16"), R("r", 0, 304)], [R("so1")])
+        scan(("so1", 0, 304), M16, ("r", 0, 304))
 
-    def list_abs(out, key):
-        S(lambda e: e.activation(out, T.so1[:, 15:304:16], F.Abs, scale=T.sc16[:, 0:1]), [R("so1"), R("sc16")], [R(key)])
+    def next_scan():
+        scan(("son", 0, 304), M16, ("r", 1, 305))
 
-    def stage_list(fill):
+    def nothing():
+        pass
+
+    def unsigned_list(ahead=nothing, between=nothing):
         own_scan()
-        scan(T.son[:, :], T.mask16[:, :], T.r[:, 1:305], [R("mask16"), R("r", 1, 305)], [R("son")])
-        fill()
-        list_abs(T.za[:, 0:19], "za")
-        V(lambda e: e.tensor_scalar(T.tmp[:, 0:19], T.son[:, 15:304:16], 0.0, float(K), A.is_gt, A.mult), [R("son")], [R("tmp")])
-        V(lambda e: e.tensor_tensor(T.yy[:, 0:19], T.za[:, 0:19], T.tmp[:, 0:19], A.add), [R("za"), R("tmp")], [R("yy")])
-        V(lambda e: e.tensor_copy(T.off[:, 0:19], T.yy[:, 0:19]), [R("yy")], [R("off")])
+        next_scan()
+        ahead()
+        act(("za", 0, 19), ("so1", 15, 304, 16), F.Abs, scale=SC16)
+        ts(("tmp", 0, 19), ("son", 15, 304, 16), 0.0, float(K), A.is_gt, A.mult)
+        between()
+        tt(("yy", 0, 19), ("za", 0, 19), ("tmp", 0, 19), A.add)
 
-    def unpack(qc, qs, keys, banks):
+    def unsigned_end():
+        ts(("off", 0, 19), ("yy", 0, 19), float(MID), None, A.add)
+
+    def signed_list():
+        next_scan()
+        own_scan()
+        ts(("tmp", 0, 19), ("son", 15, 304, 16), 0.0, ("kp", 0, 1), A.is_gt, A.mult)
+        tt(("yy", 0, 19), ("so1", 15, 304, 16), ("tmp", 0, 19), A.add)
+        ts(("off", 0, 19), ("yy", 0, 19), SC16, float(MID), A.mult, A.add)
+
+    def unpack(mv, banks):
         for b in range(4):
-            mm(banks[b], C, T.eq[:, 128 * b:128 * b + 128], T.es[:, 128 * b:128 * b + 128], [R("eq")], qc[:, :], qs[:, :], keys)
+            mm(banks[b], "e", 128 * b, [R("qe", 128 * b, 128 * b + 128)], mv, 0, C)
 
-    def pieces(buf, key, banks):
-        out = []
-        for b in range(4):
-            for hf in range(2):
-                a = hf * HC
-                out.append(lambda b=b, a=a: S(lambda e: e.activation(buf[:, 4 * a + b:4 * (a + HC):4], T.ps[:, 512 * banks[b] + a:512 * banks[b] + a + HC], F.Copy),
-                                              [R("B%d" % banks[b])], [(key + str(b), a, a + HC)]))
-        return out
+    def piece(q, buf, i, b, hf):
+        a = hf * HC
+        out, src = T[buf][:, 4 * a + b:4 * (a + HC):4], T.ps[:, 512 * i + a:512 * i + a + HC]
+        rd, wr = [R("B%d" % i)], [(buf + "_" + str(b), a, a + HC)]
+        if q == "V":
+            V(lambda e: e.tensor_copy(out, src), rd, wr)
+        else:
+            S(lambda e: e.activation(out, src, F.Copy), rd, wr)
 
-    V(lambda e: e.tensor_copy(T.sl[:, 0:18], T.sti[:, :]), [R("sti")], [R("sl", 0, 18)])
-    V(lambda e: e.tensor_copy(T.sl[:, 18:19], T.sti[:, 0:1]), [R("sti")], [R("sl", 18, 19)])
-    quant_x(0, 0, T.xin)
-    quant_x(0, 1, T.xin)
+    cp(("sl", 0, 18), ("sti", 0, 18))
+    cp(("sl", 18, 19), ("sti", 0, 1))
+    quant_x(0, 0)
+    quant_x(0, 1)
     score_half(0, 0)
     score_half(0, 1)
-    V(lambda e: e.tensor_copy(T.lab[:, 0:18], T.tai[:, :]), [R("tai")], [R("lab", 0, 18)])
-    V(lambda e: e.tensor_copy(T.lab[:, 18:36], T.tbi[:, :]), [R("tbi")], [R("lab", 18, 36)])
+    cp(("lab", 0, 18), ("tai", 0, 18))
+    cp(("lab", 18, 36), ("tbi", 0, 18))
+    ts(("kp", 1, 2), p16, 15.0, K * BIG, A.not_equal, A.mult)
+    ts(("revf", 0, 20), ("revf", 0, 20), p16, None, A.subtract)
     idsg_half(0)
+    ts(("kp", 0, 1), ("kp", 1, 2), float(K), None, A.max)
+    cp(("rev", 0, 20), ("revf", 0, 20))
     idsg_half(1)
 
     def more_constants():
-        V(lambda e: e.tensor_copy(T.ab[:, 0:18], T.tai[:, :]), [R("tai")], [R("ab", 0, 18)])
-        V(lambda e: e.tensor_copy(T.ab[:, 18:36], T.tbi[:, :]), [R("tbi")], [R("ab", 18, 36)])
-        V(lambda e: e.tensor_scalar(T.ma[:, 0:288], T.tm4[:, :], T.pf[:, 3:4], BIG, A.is_equal, A.mult), [R("tm4"), R("pf")], [R("ma")])
-        V(lambda e: e.tensor_scalar(T.mb[:, 0:288], T.tm4[:, :], T.pf[:, 2:3], None, A.not_equal), [R("tm4"), R("pf")], [R("mb")])
-        V(lambda e: e.tensor_tensor(T.mask4[:, :], T.ma[:, 0:288], T.mb[:, 0:288], A.max), [R("ma"), R("mb")], [R("mask4")])
-        V(lambda e: e.tensor_scalar(T.sc4[:, 1:2], T.pf[:, 2:3], 3.0, 1.0 / BIG, A.is_equal, A.max), [R("pf")], [R("sc4", 1, 2)])
-        V(lambda e: e.tensor_scalar(T.sc4[:, 0:1], T.sc4[:, 1:2], 4.0, None, A.mult), [R("sc4", 1, 2)], [R("sc4", 0, 1)])
-        V(lambda e: e.tensor_scalar(T.tp[:, 0:1], T.pf[:, 4:5], 508.0, None, A.add), [R("pf")], [R("tp")])
-
-    def unpackers():
-        for b in range(4):
-            V(lambda e: e.tensor_scalar(T.eb[:, 512 * b:512 * b + 512], T.ei[:, :], float(b), None, A.is_equal), [R("ei")], [R("eb", b, b + 1)])
-        V(lambda e: e.quantize_mx(T.eq[:, :], T.es[:, :], T.eb[:, :]), [R("eb", 0, 4)], [R("eq")])
+        cp(("ab", 0, 18), ("tai", 0, 18))
+        cp(("ab", 18, 36), ("tbi", 0, 18))
+        ts(M4, ("tm4", 0, 288), p4, UP, A.not_equal, A.mult)
+        for k in range(3):
+            ts(("sc4", k, k + 1), p4, k + 1.0, 1.0 / UP, A.is_ge, A.max)
+        tt(("sc4", 3, 4), ("sc4", 0, 1), ("sc4", 1, 2), A.mult)
+        ts(SC4, ("sc4", 3, 4), ("sc4", 2, 3), 4.0, A.mult, A.mult)
 
     def differences():
-        V(lambda e: e.tensor_tensor(T.dd[:, 0:18], T.ab[:, 18:36], T.ab[:, 0:18], A.subtract), [R("ab")], [R("dd", 0, 18)])
-        V(lambda e: e.tensor_tensor(T.dd[:, 18:36], T.ab[:, 0:18], T.ab[:, 18:36], A.subtract), [R("ab")], [R("dd", 18, 36)])
+        tt(("dd", 0, 18), ("ab", 18, 36), ("ab", 0, 18), A.subtract)
+        tt(("dd", 18, 36), ("ab", 0, 18), ("ab", 18, 36), A.subtract)
 
     for r in range(3):
         partner = T.cores[rank ^ STEP[r]]
@@ -298,117 +327,140 @@ def rank_program(g, core, T, topo):
         engines = topo.engines(core, partner)[:8]
         mask = sum(1 << e for e in engines)
         ne = len(engines)
-        qc, qs = T["qx%d" % r], T["sx%d" % r]
-        lc, ls = T["lq%d" % r], T["lsx%d" % r]
-        own, arr = T["own%d" % r], T["arr%d" % r]
+        qx, lx, own, arr = "x%d" % r, "l%d" % r, "own%d" % r, "arr%d" % r
 
-        before("P", [R("qx%d" % r)])
-        g.remote_dma(lc[:, :].bitcast(dt.uint8), qc[:, :].bitcast(dt.uint8), T.sem["ax%d" % r], T.sem.left, pid, rid, mask)
-        g.remote_dma(ls[:, :], qs[:, :], T.sem["ax%d" % r], T.sem.left, pid, rid, mask)
+        before("P", [R("q" + qx)])
+        g.remote_dma(T["q" + lx][:, :].bitcast(dt.uint8), T["q" + qx][:, :].bitcast(dt.uint8), T.sem["ax%d" % r], T.sem.left, pid, rid, mask)
+        g.remote_dma(T["p" + lx][:, :], T["p" + qx][:, :], T.sem["ax%d" % r], T.sem.left, pid, rid, mask)
         count["left"] = count.get("left", 0) + 2 * ne
-        arrival("ax%d" % r, 2 * ne, [R("lq%d" % r)])
-        arrival("al%d" % r, ne, [R("arr%d" % r)])
+        arrival("ax%d" % r, 2 * ne, [R("q" + lx)])
+        arrival("al%d" % r, ne, [R(arr)])
         if r == 0:
-            P(T.idf[:, :], [[1, 288]], 0, 0, "idf", True)
+            iota(("idf", 0, 288), [[1, 288]], 0, 0)
+            unpacker(2)
+            unpacker(3)
 
         stage_gather(0)
-        stage_list(lambda: table("S", "A", 1))
-        table("S", "A", 0)
-        table("S", "B", 1)
-        table("V", "B", 0)
-        if r == 0:
-            unpackers()
-            more_constants()
-            differences()
-        unpack(qc, qs, [R("qx%d" % r)], [2, 3, 4, 5])
-        unpack(lc, ls, [R("lq%d" % r)], [6, 7, 0, 1])
-        todo = pieces(T.tt, "tt", [2, 3, 4, 5]) + pieces(T.tq, "tq", [6, 7, 0, 1])
+        unsigned_list(lambda: table("S", "w", "idsg", True, True), nothing if r else more_constants)
+        table("S", "w", "idsg", True, False)
+        table("S", "w", "idsg", False, True)
+        table("V", "w", "idsg", False, False)
+        unsigned_end()
+        own_t, got_t = [2, 3, 4, 5], [6, 7, 0, 1]
+        if r:
+            unpack(qx, own_t)
+            unpack(lx, got_t)
+        own_p = [(b, hf) for b in range(4) for hf in range(2)]
 
-        for t in range(1, STAGES + 1):
+        def own_pieces(n):
+            for i in range(n):
+                b, hf = own_p.pop(0)
+                piece("S", "tt", own_t[b], b, hf)
+
+        for t in range(1, STAGES):
             stage_gather(t)
-            if t < STAGES:
-                stage_list(todo.pop(0))
-                todo.pop(0)()
-        scan(T.so4[:, :], T.mask4[:, :], T.r[:, 0:288], [R("mask4"), R("r", 0, 288)], [R("so4")])
-        S(lambda e: e.activation(T.z4[:, :], T.so4[:, 3:288:4], F.Abs, scale=T.sc4[:, 0:1]), [R("so4"), R("sc4", 0, 1)], [R("z4")])
-        V(lambda e: e.tensor_scalar(T.t4[:, :], T.z4[:, :], 1024.0, -0.5, A.max, A.mult), [R("z4")], [R("t4")])
-        V(lambda e: e.tensor_tensor(T.y4[:, :], T.z4[:, :], T.t4[:, :], A.add), [R("z4"), R("t4")], [R("y4")])
-        V(lambda e: e.tensor_scalar(own[:, :], T.y4[:, :], T.tp[:, 0:1], None, A.add), [R("y4"), R("tp")], [R("own%d" % r)])
-        before("P", [R("own%d" % r)])
-        g.remote_dma(arr[:, :], own[:, :], T.sem["al%d" % r], T.sem.left, pid, rid, mask)
+            if r == 0 and t <= 4:
+                quant("e", 128 * t - 128, 128 * t, "eb", [R("eb", t - 1, t)])
+                if t == 4:
+                    unpack(qx, own_t)
+                    unpack(lx, got_t)
+            if t == 1:
+                unsigned_list()
+                unsigned_end()
+                mirror(True)
+            elif t == 2:
+                mirror(False)
+                signed_list()
+                differences()
+            elif t == 6:
+                unsigned_list(lambda: own_pieces(2))
+                own_pieces(2)
+                unsigned_end()
+            else:
+                if t < 5:
+                    table("S", "wl", "idf", t == 3, False)
+                else:
+                    table("S", "wl", "idf", True, True)
+                    table("S", "wl", "idf", False, True)
+                    own_pieces(2)
+                signed_list()
+        stage_gather(STAGES)
+        own_pieces(2)
+        scan(("so4", 0, 288), M4, ("rl", 0, 288))
+        scan(("sol", 0, 304), M16, ("rl", 0, 304))
+        ts((own, 0, 72), ("so4", 3, 288, 4), SC4, t4, A.mult, A.add)
+        before("P", [R(own)])
+        g.remote_dma(T[arr][:, :], T[own][:, :], T.sem["al%d" % r], T.sem.left, pid, rid, mask)
         count["left"] += ne
-        while todo:
-            todo.pop(0)()
 
-        ok = R("own%d" % r)
-        vgather(T.zt[:, 0:576], T.tt[:, 0:1152], own[:, 0:36], lanes("tt") + [ok], [R("zt", 0, HC)])
-        sgather(T.zt[:, 576:1152], T.tt[:, 0:1152], own[:, 36:72], lanes("tt") + [ok], [R("zt", HC, C)])
-        own_scan()
-        list_abs(T.zs[:, 0:19], "zs")
-        V(lambda e: e.tensor_scalar(T.ts[:, 0:18], T.zs[:, 0:18], 256.0, -0.5, A.max, A.mult), [R("zs")], [R("ts")])
-        V(lambda e: e.tensor_tensor(T.ys[:, 0:18], T.zs[:, 0:18], T.ts[:, 0:18], A.add), [R("zs"), R("ts")], [R("ys")])
-        V(lambda e: e.tensor_scalar(T.sl[:, 0:18], T.ys[:, 0:18], 127.0, None, A.add), [R("ys")], [R("sl", 0, 18)])
-        V(lambda e: e.tensor_scalar(T.sl[:, 18:19], T.ys[:, 0:1], 127.0, None, A.add), [R("ys")], [R("sl", 18, 19)])
-        if r == 0:
-            V(lambda e: e.quantize_mx(T.vq[:, :], T.vs[:, :], T.vt[:, :]), [R("vt")], [R("vq")])
-
-        ak = R("arr%d" % r)
-        vgather(T.zp[:, 0:576], T.tq[:, 0:1152], arr[:, 0:36], lanes("tq") + [ak], [R("zp", 0, HC)])
-        sgather(T.zp[:, 576:1152], T.tq[:, 0:1152], arr[:, 36:72], lanes("tq") + [ak], [R("zp", HC, C)])
+        gather("S", ("zt", 576, 1152), ("tt", 0, 1152), (own, 36, 72), [R("zt", HC, C)], lanes("tt"))
+        ts(("sl", 0, 18), ("sol", 15, 288, 16), SC16, None, A.mult)
+        ts(("sl", 18, 19), ("sol", 15, 16), SC16, None, A.mult)
+        gather("V", ("zt", 0, 576), ("tt", 0, 1152), (own, 0, 36), [R("zt", 0, HC)], lanes("tt"))
         for hf in range(2):
-            a, b = hf * HC, hf * HC + HC
-            V(lambda e: e.quantize_mx(T.zq[:, a:b], T.zqs[:, a:b], T.zp[:, 4 * a:4 * b]), [R("zp", a, b)], [R("zq", a, b)])
+            for b in (0, 1):
+                piece("S", "tq", got_t[b], b, hf)
+                piece("V", "tq", got_t[b + 2], b + 2, hf)
+        if r == 0:
+            quant("v", 0, 128, "vt", [R("vt")])
+
+        for hf in range(2):
+            c = 36 * hf
+            a, m, b = hf * HC, hf * HC + HC // 2, hf * HC + HC
+            gather("V", ("zp", 4 * a, 4 * m), ("tq", 0, 1152), (arr, c, c + 18), [R("zp", a, m)], lanes("tq"))
+            gather("S", ("zp", 4 * m, 4 * b), ("tq", 0, 1152), (arr, c + 18, c + 36), [R("zp", m, b)], lanes("tq"))
+            quant("z", a, b, "zp", [R("zp", a, b)])
             for k in (0, 2, 1, 3):
-                mm(4 * hf + k, HC, T.wq[:, 128 * k:128 * k + 128], T.wsc[:, 128 * k:128 * k + 128], [R("wq"), R("wsc")], T.zq[:, a:b], T.zqs[:, a:b], [R("zq", a, b)])
+                mm(4 * hf + k, "w", 128 * k, [R("qw"), R("pw")], "z", a, b)
         for hf in range(2):
             a, b = hf * HC, hf * HC + HC
             for k in (0, 2, 1, 3):
                 i = 4 * hf + k
-                out = T.h[:, 4 * a + k:4 * b:4]
+                out, wr = T.h[:, 4 * a + k:4 * b:4], [("h_%d" % k, a, b)]
                 if k < 2:
-                    V(lambda e: e.tensor_scalar(out, bank(i, HC), 0.03125, None, A.mult), [R("B%d" % i)], [("h%d" % k, a, b)])
+                    V(lambda e: e.tensor_scalar(out, bank(i, HC), 0.03125, None, A.mult), [R("B%d" % i)], wr)
                 else:
-                    S(lambda e: e.activation(out, bank(i, HC), F.Copy, scale=0.03125), [R("B%d" % i)], [("h%d" % k, a, b)])
+                    S(lambda e: e.activation(out, bank(i, HC), F.Copy, scale=0.03125), [R("B%d" % i)], wr)
 
-        V(lambda e: e.quantize_mx(T.hq[:, :], T.hqs[:, :], T.h[:, :]), lanes("h"), [R("hq")])
-        mm(2, C, T.ur[:, :], T.urs[:, :], [R("ur"), R("urs")], T.hq[:, :], T.hqs[:, :], [R("hq")])
-        S(lambda e: e.activation(T.cs[:, :], bank(2, C), F.Sign, bias=TINY), [R("B2")], [R("cs")])
-        xt, xk = T["xt%d" % (r + 1)], "xt%d" % (r + 1)
+        quant("h", 0, C, "h", lanes("h"))
+        mm(2, "ur", 0, ukeys, "h", 0, C)
+        S(lambda e: e.activation(T.cs[:, :], bank(2, C), F.Sign, bias=TINY), [R("B2")], [R("cs", 0, C)])
+        xt = "xt%d" % (r + 1)
 
         def new_half(hf):
             a, b = hf * HC, hf * HC + HC
-            V(lambda e: e.tensor_tensor(xt[:, 4 * a:4 * b], T.h[:, 0:1152].indirect(arr[:, 36 * hf:36 * hf + 36]), T.zt[:, 4 * a:4 * b], A.add),
-              lanes("h") + [ak, R("zt", a, b)], [R(xk, a, b)])
+            V(lambda e: e.tensor_tensor(T[xt][:, 4 * a:4 * b], T.h[:, 0:1152].indirect(T[arr][:, 36 * hf:36 * hf + 36]), T.zt[:, 4 * a:4 * b], A.add),
+              lanes("h") + [R(arr), R("zt", a, b)], [R(xt, a, b)])
         new_half(0)
-        quant_x(r + 1, 0, xt)
-        scan(T.soc[:, :], T.mask16[:, 0:288], T.cs[:, :], [R("mask16"), R("cs")], [R("soc")])
-        V(lambda e: e.tensor_scalar(T.c01[:, :], T.soc[:, 15:288:16], 0.0, None, A.is_gt), [R("soc")], [R("c01")])
-        V(lambda e: e.tensor_tensor(T.m2[:, 0:18], T.dd[:, 0:18], T.c01[:, :], A.mult), [R("dd", 0, 18), R("c01")], [R("m2", 0, 18)])
-        V(lambda e: e.tensor_tensor(T.m2[:, 18:36], T.dd[:, 18:36], T.c01[:, :], A.mult), [R("dd", 18, 36), R("c01")], [R("m2", 18, 36)])
-        V(lambda e: e.tensor_tensor(T.ab[:, :], T.ab[:, :], T.m2[:, :], A.add), [R("ab"), R("m2", 0, 36)], [R("ab")])
-        V(lambda e: e.tensor_copy(T.lab[:, :], T.ab[:, :]), [R("ab")], [R("lab", 0, 36)])
+        scan(("soc", 0, 288), ("mask16", 0, 288), ("cs", 0, 288))
+        quant_x(r + 1, 0)
+        ts(("c01", 0, 18), ("soc", 15, 288, 16), 0.0, None, A.is_gt)
+        new_half(1)
+        tt(("m2", 0, 18), ("dd", 0, 18), ("c01", 0, 18), A.mult)
+        tt(("m2", 18, 36), ("dd", 18, 36), ("c01", 0, 18), A.mult)
+        quant_x(r + 1, 1)
+        tt(("ab", 0, 36), ("ab", 0, 36), ("m2", 0, 36), A.add)
         if r < 2:
             score_half(r + 1, 0)
-        else:
-            for i in range(3):
-                lo, lk = (T.sl[:, 0:18], "sl") if i == 0 else (T.lab[:, 18 * i - 18:18 * i], "lab")
-                sgather(T.opr[:, C * i:C * i + C], T.idf[:, 0:C], lo, [R("idf"), R(lk)], [R("opr", i, i + 1)])
-            op("Y", lambda e: e.dma_start(T.op[:, :], T.opr[0:128:16, :]), [R("opr", 0, 3)], [], dma=True)
-        new_half(1)
-        quant_x(r + 1, 1, xt)
-        if r < 2:
-            score_half(r + 1, 1)
             idsg_half(0)
+            cp(("lab", 0, 36), ("ab", 0, 36))
+            score_half(r + 1, 1)
             idsg_half(1)
-            differences()
+        else:
+            cp(("lab", 0, 36), ("ab", 0, 36))
 
+    def out(q, dst, src, rd):
+        op(q, lambda e: e.dma_start(dst, src), rd, [], dma=True)
     for hf in range(2):
-        a, b = hf * HC, hf * HC + HC
-        mm(3 + hf, HC, T.vq[:, :], T.vs[:, :], [R("vq")], T.qx3[:, a:b], T.sx3[:, a:b], [R("qx3", a, b)])
+        mm(3 + hf, "v", 0, [R("qv")], "x3", hf * HC, hf * HC + HC)
+    out("Y", T.oc[:, :], T.qx3[:, :].bitcast(dt.uint8), [R("qx3")])
+    gather("S", ("opr", 0, C), ("idf", 0, C), ("sl", 0, 18))
     V(lambda e: e.tensor_copy(T.yo[:, 0:HC], bank(3, HC)), [R("B3")], [R("yo", 0, HC)])
-    op("Y", lambda e: e.dma_start(T.oc[:, :], T.qx3[:, :].bitcast(dt.uint8)), [R("qx3")], [], dma=True)
+    V(lambda e: e.tensor_copy(T.yo[:, HC:C], bank(4, HC)), [R("B4")], [R("yo", HC, C)])
+    gather("V", ("opr", C, 2 * C), ("idf", 0, C), ("lab", 0, 18))
+    gather("S", ("opr", 2 * C, 3 * C), ("idf", 0, C), ("lab", 18, 36))
+    out("Y", T.y[:, :], T.yo[:, :], [R("yo")])
     for k in range(4):
-        op("Y", lambda e: e.dma_start(T.osc[4 * k:4 * k + 4, :], T.sx3[32 * k:32 * k + 4, :]), [R("qx3")], [], dma=True)
-    S(lambda e: e.activation(T.yo[:, HC:C], bank(4, HC), F.Copy), [R("B4")], [R("yo", HC, C)])
-    op("S", lambda e: e.dma_start(T.y[:, :], T.yo[:, :]), [R("yo")], [], dma=True)
+        out("S" if k % 2 else "Y", T.osc[4 * k:4 * k + 4, :], T.px3[32 * k:32 * k + 4, :], [R("qx3")])
+    out("S", T.op[:, :], T.opr[0:128:16, :], [R("opr")])
     finish()

@@ -5,6 +5,7 @@ STEP = [4, 1, 2]
 STAGES = 7
 C = 288
 HC = C // 2
+PART = [(0, 160), (160, 288)]
 MID = 336
 K = 672
 BIG = 2.0 ** 40
@@ -26,7 +27,7 @@ for _n, _c in [("u", 128), ("ur", 128), ("v", 128), ("w", 512), ("e", 512), ("z"
     SCRATCH["q" + _n] = ("sbuf", [128, _c], "float8_e4m3fn_x4")
     SCRATCH["p" + _n] = ("sbuf", [128, _c], "uint8")
 _bufs("sbuf", "int32", pi=8, pk=8, offui=8, tai=18, tbi=18, sti=18)
-_bufs("sbuf", "float32", pf=8, sc16=8, kp=8, sc4=8, tp=8, revf=20, idf=288, ab=36, dd=36, m2=36, c01=18, za=20, tmp=20, yy=20,
+_bufs("sbuf", "float32", pf=8, sc16=8, kp=8, sc4=8, revf=20, idf=288, ab=36, dd=36, m2=36, c01=18, za=20, tmp=20, yy=20,
       wl=1344, rl=304, so4=288, sol=304, opr=864, yo=288)
 _bufs("sbuf", "uint16", offu=8, rev=20, sl=20, lab=36, off=20, own0=72, own1=72, own2=72, arr0=72, arr1=72, arr2=72)
 
@@ -158,9 +159,12 @@ def rank_program(g, core, T, topo):
 
     def load(q, dst, src, key, a=0, b=100000):
         op(q, lambda e: e.dma_start(dst, src), [], [(key, a, b)], dma=True)
-    load("Y", T.xin[:, 0:576], T.x[:, 0:576], "xin", 0, HC)
+
+    def load_x(a, b):
+        load("Y", T.xin[:, 4 * a:4 * b], T.x[:, 4 * a:4 * b], "xin", a, b)
+    load_x(*PART[0])
     load("S", T.ut[:, :], T.u[:, :], "ut")
-    load("Y", T.xin[:, 576:1152], T.x[:, 576:1152], "xin", HC, C)
+    load_x(*PART[1])
     load("Y", T.sti[:, :], T.st[:, :], "sti")
     load("S", T.tai[:, :], T.ta[:, :], "tai")
     load("S", T.tbi[:, :], T.tb[:, :], "tbi")
@@ -174,17 +178,18 @@ def rank_program(g, core, T, topo):
     iota(("pi", 0, 5), [[1, 5]], 0, 1, False)
     iota(("offui", 0, 8), [[16, 8]], 0, 0, False)
     iota(("tm", 0, 304), [[0, 19], [1, 16]], 0, 0)
+    iota(("revf", 0, 20), [[-16, 20]], 320, 0)
     iota(("enc", 0, 256), [[1, 256]], 1, 0)
     iota(("enc", 256, 288), [[2, 32]], 258, 0)
-    iota(("revf", 0, 20), [[-16, 20]], 320, 0)
     iota(("tm4", 0, 288), [[0, 72], [1, 4]], 0, 0)
+
+    def fill(win, a, b):
+        act((win, a, b), ("ones", 0, b - a), F.Copy)
 
     V(lambda e: e.memset(T.ones[:, :], 1.0), [], [R("ones", 0, 512)])
     V(lambda e: e.memset(T.r[:, 304:320], 1.0), [], [R("r", 304, 320)])
-    for win in ("w", "wl"):
-        for a in (0, 512, 1024):
-            b = min(a + 512, 1344)
-            act((win, a, b), ("ones", 0, b - a), F.Copy)
+    for a in (0, 448, 896):
+        fill("w", a, a + 448)
     unpacker(0)
     unpacker(1)
     for j, (src, sh, an) in enumerate([(0, 0, 15), (1, 0, 15), (0, 2, 3), (0, 0, 3)]):
@@ -198,14 +203,19 @@ def rank_program(g, core, T, topo):
     ts(("ma", 0, 304), ("tm", 0, 304), q16, BIG, A.is_equal, A.mult)
     ts(("mb", 0, 304), ("tm", 0, 304), p16, None, A.not_equal)
     ts(("sc16", 0, 1), p16, 15.0, 1.0 / BIG, A.is_equal, A.max)
+    ts(("kp", 1, 2), p16, 15.0, K * BIG, A.not_equal, A.mult)
     tt(("mask16", 0, 304), ("ma", 0, 304), ("mb", 0, 304), A.max)
+    ts(("revf", 0, 20), ("revf", 0, 20), p16, None, A.subtract)
+    ts(("kp", 0, 1), ("kp", 1, 2), float(K), None, A.max)
     quant("u", 0, 128, "ut", [R("ut")])
+    cp(("rev", 0, 20), ("revf", 0, 20))
     V(lambda e: e.tensor_copy(T.qur[:, 0:128].bitcast(dt.uint32), T.qu[:, 0:128].bitcast(dt.uint32).indirect(T.offu[:, 0:8])), [R("qu"), R("offu")], [R("qur", 0, 1)])
-    V(lambda e: e.tensor_copy(T.pur[:, 0:128], T.pu[:, 0:128].indirect(T.offu[:, 0:8])), [R("qu"), R("offu")], [R("qur", 1, 2)])
+    S(lambda e: e.activation(T.pur[:, 0:128], T.pu[:, 0:128].indirect(T.offu[:, 0:8]), F.Copy), [R("qu"), R("offu")], [R("qur", 1, 2)])
 
     def quant_x(r, hf):
         src = "xt%d" % r if r else "xin"
-        quant("x%d" % r, hf * HC, hf * HC + HC, src, [R(src, hf * HC, hf * HC + HC)])
+        a, b = PART[hf]
+        quant("x%d" % r, a, b, src, [R(src, a, b)])
 
     def bank(i, n):
         return T.ps[:, 512 * i:512 * i + n]
@@ -216,28 +226,28 @@ def rank_program(g, core, T, topo):
 
     ukeys = [R("qur", 0, 2)]
 
-    def score_half(r, hf):
-        a, b = hf * HC, hf * HC + HC
+    def score_part(r, hf):
+        a, b = PART[hf]
         mm(hf, "ur", 0, ukeys, "x%d" % r, a, b)
-        S(lambda e: e.activation(T.sg[:, a:b], bank(hf, HC), F.Sign, bias=TINY), [R("B%d" % hf)], [R("sg", a, b)])
+        S(lambda e: e.activation(T.sg[:, a:b], bank(hf, b - a), F.Sign, bias=TINY), [R("B%d" % hf)], [R("sg", a, b)])
 
-    def idsg_half(hf):
-        a, b = hf * HC, hf * HC + HC
+    def idsg_part(hf):
+        a, b = PART[hf]
         tt(("idsg", a, b), ("sg", a, b), ("enc", a, b), A.mult)
 
     def scan(out, mask, row):
         V(lambda e: e.tensor_tensor_scan(ap(out), ap(mask), ap(row), 0.0, A.mult, A.add), rgs(mask, row), rgs(out))
 
-    def table(q, dst, src, first, tail):
-        m, c = (MID, 0) if first else (MID + K, 18)
-        if tail:
-            gather(q, (dst, m + 258, m + 321, 2), (src, 0, C), ("lab", c + 16, c + 18))
+    def table(q, dst, src, first, c, d):
+        m, o = (MID, 0) if first else (MID + K, 18)
+        if c == 16:
+            gather(q, (dst, m + 258, m + 321, 2), (src, 0, C), ("lab", o + c, o + d))
         else:
-            gather(q, (dst, m + 1, m + 257), (src, 0, C), ("lab", c, c + 16))
+            gather(q, (dst, m + 1 + 16 * c, m + 1 + 16 * d), (src, 0, C), ("lab", o + c, o + d))
 
-    def mirror(first):
+    def mirror(win, first):
         m = MID if first else MID + K
-        gather("S", ("w", m - 320, m), ("w", m, m + 336), ("rev", 0, 20))
+        gather("S", (win, m - 320, m), (win, m, m + 336), ("rev", 0, 20))
 
     VC = 10
 
@@ -261,11 +271,12 @@ def rank_program(g, core, T, topo):
     def nothing():
         pass
 
-    def unsigned_list(ahead=nothing, between=nothing):
+    def unsigned_list(scalar=nothing, vector=nothing, between=nothing):
         own_scan()
         next_scan()
-        ahead()
+        scalar()
         act(("za", 0, 19), ("so1", 15, 304, 16), F.Abs, scale=SC16)
+        vector()
         ts(("tmp", 0, 19), ("son", 15, 304, 16), 0.0, float(K), A.is_gt, A.mult)
         between()
         tt(("yy", 0, 19), ("za", 0, 19), ("tmp", 0, 19), A.add)
@@ -273,16 +284,16 @@ def rank_program(g, core, T, topo):
     def unsigned_end():
         ts(("off", 0, 19), ("yy", 0, 19), float(MID), None, A.add)
 
-    def signed_list():
+    def signed_list(between=nothing):
         next_scan()
         own_scan()
         ts(("tmp", 0, 19), ("son", 15, 304, 16), 0.0, ("kp", 0, 1), A.is_gt, A.mult)
+        between()
         tt(("yy", 0, 19), ("so1", 15, 304, 16), ("tmp", 0, 19), A.add)
         ts(("off", 0, 19), ("yy", 0, 19), SC16, float(MID), A.mult, A.add)
 
-    def unpack(mv, banks):
-        for b in range(4):
-            mm(banks[b], "e", 128 * b, [R("qe", 128 * b, 128 * b + 128)], mv, 0, C)
+    def unpack_lane(mv, i, b):
+        mm(i, "e", 128 * b, [R("qe", 128 * b, 128 * b + 128)], mv, 0, C)
 
     def piece(q, buf, i, b, hf):
         a = hf * HC
@@ -297,25 +308,27 @@ def rank_program(g, core, T, topo):
     cp(("sl", 18, 19), ("sti", 0, 1))
     quant_x(0, 0)
     quant_x(0, 1)
-    score_half(0, 0)
-    score_half(0, 1)
+    score_part(0, 0)
+    score_part(0, 1)
     cp(("lab", 0, 18), ("tai", 0, 18))
     cp(("lab", 18, 36), ("tbi", 0, 18))
-    ts(("kp", 1, 2), p16, 15.0, K * BIG, A.not_equal, A.mult)
-    ts(("revf", 0, 20), ("revf", 0, 20), p16, None, A.subtract)
-    idsg_half(0)
-    ts(("kp", 0, 1), ("kp", 1, 2), float(K), None, A.max)
-    cp(("rev", 0, 20), ("revf", 0, 20))
-    idsg_half(1)
+    idsg_part(0)
+    idsg_part(1)
 
-    def more_constants():
-        cp(("ab", 0, 18), ("tai", 0, 18))
-        cp(("ab", 18, 36), ("tbi", 0, 18))
-        ts(M4, ("tm4", 0, 288), p4, UP, A.not_equal, A.mult)
-        for k in range(3):
-            ts(("sc4", k, k + 1), p4, k + 1.0, 1.0 / UP, A.is_ge, A.max)
-        tt(("sc4", 3, 4), ("sc4", 0, 1), ("sc4", 1, 2), A.mult)
-        ts(SC4, ("sc4", 3, 4), ("sc4", 2, 3), 4.0, A.mult, A.mult)
+    def sc4_factor(k):
+        ts(("sc4", k, k + 1), p4, k + 1.0, 1.0 / UP, A.is_ge, A.max)
+
+    def later(t):
+        if t == 2:
+            ts(M4, ("tm4", 0, 288), p4, UP, A.not_equal, A.mult)
+        elif t == 3:
+            sc4_factor(0)
+            sc4_factor(1)
+        elif t == 4:
+            sc4_factor(2)
+            tt(("sc4", 3, 4), ("sc4", 0, 1), ("sc4", 1, 2), A.mult)
+        elif t == 5:
+            ts(SC4, ("sc4", 3, 4), ("sc4", 2, 3), 4.0, A.mult, A.mult)
 
     def differences():
         tt(("dd", 0, 18), ("ab", 18, 36), ("ab", 0, 18), A.subtract)
@@ -328,6 +341,7 @@ def rank_program(g, core, T, topo):
         mask = sum(1 << e for e in engines)
         ne = len(engines)
         qx, lx, own, arr = "x%d" % r, "l%d" % r, "own%d" % r, "arr%d" % r
+        own_t, got_t = [2, 3, 4, 5], [6, 7, 0, 1]
 
         before("P", [R("q" + qx)])
         g.remote_dma(T["q" + lx][:, :].bitcast(dt.uint8), T["q" + qx][:, :].bitcast(dt.uint8), T.sem["ax%d" % r], T.sem.left, pid, rid, mask)
@@ -340,16 +354,20 @@ def rank_program(g, core, T, topo):
             unpacker(2)
             unpacker(3)
 
+        def tails():
+            table("S", "w", "idsg", True, 16, 18)
+            table("S", "w", "idsg", False, 16, 18)
         stage_gather(0)
-        unsigned_list(lambda: table("S", "w", "idsg", True, True), nothing if r else more_constants)
-        table("S", "w", "idsg", True, False)
-        table("S", "w", "idsg", False, True)
-        table("V", "w", "idsg", False, False)
+        unsigned_list(tails, lambda: table("V", "w", "idsg", False, 0, 6))
+        table("S", "w", "idsg", True, 0, 16)
+        table("S", "w", "idsg", False, 12, 16)
+        table("V", "w", "idsg", False, 6, 12)
         unsigned_end()
-        own_t, got_t = [2, 3, 4, 5], [6, 7, 0, 1]
         if r:
-            unpack(qx, own_t)
-            unpack(lx, got_t)
+            for b in range(4):
+                unpack_lane(qx, own_t[b], b)
+            for b in range(4):
+                unpack_lane(lx, got_t[b], b)
         own_p = [(b, hf) for b in range(4) for hf in range(2)]
 
         def own_pieces(n):
@@ -357,46 +375,64 @@ def rank_program(g, core, T, topo):
                 b, hf = own_p.pop(0)
                 piece("S", "tt", own_t[b], b, hf)
 
+        def plain_tails():
+            table("S", "wl", "idf", True, 16, 18)
+            table("S", "wl", "idf", False, 16, 18)
+
         for t in range(1, STAGES):
             stage_gather(t)
-            if r == 0 and t <= 4:
-                quant("e", 128 * t - 128, 128 * t, "eb", [R("eb", t - 1, t)])
-                if t == 4:
-                    unpack(qx, own_t)
-                    unpack(lx, got_t)
+            mine = nothing
+            if r == 0:
+                mine = lambda: later(t)
+                if t == 1:
+                    cp(("ab", 0, 18), ("tai", 0, 18))
+                    cp(("ab", 18, 36), ("tbi", 0, 18))
+                elif t <= 5:
+                    b = t - 2
+                    quant("e", 128 * b, 128 * b + 128, "eb", [R("eb", b, b + 1)])
+                    unpack_lane(qx, own_t[b], b)
+                    if b == 3:
+                        for b in range(4):
+                            unpack_lane(lx, got_t[b], b)
             if t == 1:
-                unsigned_list()
+                unsigned_list(nothing if r else lambda: fill("wl", 0, 336))
                 unsigned_end()
-                mirror(True)
+                mirror("w", True)
             elif t == 2:
-                mirror(False)
-                signed_list()
+                mirror("w", False)
+                if r == 0:
+                    fill("wl", 336, 672)
+                signed_list(mine)
                 differences()
-            elif t == 6:
+            elif t == 6 and r == 0:
                 unsigned_list(lambda: own_pieces(2))
                 own_pieces(2)
                 unsigned_end()
             else:
                 if t < 5:
-                    table("S", "wl", "idf", t == 3, False)
-                else:
-                    table("S", "wl", "idf", True, True)
-                    table("S", "wl", "idf", False, True)
+                    if r == 0:
+                        fill("wl", 336 * t - 336, 336 * t)
+                    table("S", "wl", "idf", t == 3, 0, 16)
+                elif r:
+                    mirror("wl", t == 5)
+                if t == (4 if r else 5):
+                    plain_tails()
+                if t == 5 or r and t != 4:
                     own_pieces(2)
-                signed_list()
+                signed_list(mine)
         stage_gather(STAGES)
         own_pieces(2)
         scan(("so4", 0, 288), M4, ("rl", 0, 288))
-        scan(("sol", 0, 304), M16, ("rl", 0, 304))
         ts((own, 0, 72), ("so4", 3, 288, 4), SC4, t4, A.mult, A.add)
         before("P", [R(own)])
         g.remote_dma(T[arr][:, :], T[own][:, :], T.sem["al%d" % r], T.sem.left, pid, rid, mask)
         count["left"] += ne
 
         gather("S", ("zt", 576, 1152), ("tt", 0, 1152), (own, 36, 72), [R("zt", HC, C)], lanes("tt"))
+        scan(("sol", 0, 304), M16, ("rl", 0, 304))
+        gather("V", ("zt", 0, 576), ("tt", 0, 1152), (own, 0, 36), [R("zt", 0, HC)], lanes("tt"))
         ts(("sl", 0, 18), ("sol", 15, 288, 16), SC16, None, A.mult)
         ts(("sl", 18, 19), ("sol", 15, 16), SC16, None, A.mult)
-        gather("V", ("zt", 0, 576), ("tt", 0, 1152), (own, 0, 36), [R("zt", 0, HC)], lanes("tt"))
         for hf in range(2):
             for b in (0, 1):
                 piece("S", "tq", got_t[b], b, hf)
@@ -405,58 +441,73 @@ def rank_program(g, core, T, topo):
             quant("v", 0, 128, "vt", [R("vt")])
 
         for hf in range(2):
-            c = 36 * hf
-            a, m, b = hf * HC, hf * HC + HC // 2, hf * HC + HC
-            gather("V", ("zp", 4 * a, 4 * m), ("tq", 0, 1152), (arr, c, c + 18), [R("zp", a, m)], lanes("tq"))
-            gather("S", ("zp", 4 * m, 4 * b), ("tq", 0, 1152), (arr, c + 18, c + 36), [R("zp", m, b)], lanes("tq"))
+            a, b = PART[hf]
+            m = (a + b) // 2
+            gather("V", ("zp", 4 * a, 4 * m), ("tq", 0, 1152), (arr, a // 4, m // 4), [R("zp", a, m)], lanes("tq"))
+            gather("S", ("zp", 4 * m, 4 * b), ("tq", 0, 1152), (arr, m // 4, b // 4), [R("zp", m, b)], lanes("tq"))
             quant("z", a, b, "zp", [R("zp", a, b)])
             for k in (0, 2, 1, 3):
                 mm(4 * hf + k, "w", 128 * k, [R("qw"), R("pw")], "z", a, b)
         for hf in range(2):
-            a, b = hf * HC, hf * HC + HC
+            a, b = PART[hf]
             for k in (0, 2, 1, 3):
                 i = 4 * hf + k
                 out, wr = T.h[:, 4 * a + k:4 * b:4], [("h_%d" % k, a, b)]
                 if k < 2:
-                    V(lambda e: e.tensor_scalar(out, bank(i, HC), 0.03125, None, A.mult), [R("B%d" % i)], wr)
+                    V(lambda e: e.tensor_scalar(out, bank(i, b - a), 0.03125, None, A.mult), [R("B%d" % i)], wr)
                 else:
-                    S(lambda e: e.activation(out, bank(i, HC), F.Copy, scale=0.03125), [R("B%d" % i)], wr)
+                    S(lambda e: e.activation(out, bank(i, b - a), F.Copy, scale=0.03125), [R("B%d" % i)], wr)
 
+        xt, last = "xt%d" % (r + 1), r == 2
+
+        def new_part(hf):
+            a, b = PART[hf]
+            V(lambda e: e.tensor_tensor(T[xt][:, 4 * a:4 * b], T.h[:, 0:1152].indirect(T[arr][:, a // 4:b // 4]), T.zt[:, 4 * a:4 * b], A.add),
+              lanes("h") + [R(arr), R("zt", a, b)], [R(xt, a, b)])
+
+        def change_scan():
+            scan(("soc", 0, 288), ("mask16", 0, 288), ("cs", 0, 288))
+
+        def change():
+            ts(("c01", 0, 18), ("soc", 15, 288, 16), 0.0, None, A.is_gt)
+        if not last:
+            new_part(0)
         quant("h", 0, C, "h", lanes("h"))
         mm(2, "ur", 0, ukeys, "h", 0, C)
         S(lambda e: e.activation(T.cs[:, :], bank(2, C), F.Sign, bias=TINY), [R("B2")], [R("cs", 0, C)])
-        xt = "xt%d" % (r + 1)
-
-        def new_half(hf):
-            a, b = hf * HC, hf * HC + HC
-            V(lambda e: e.tensor_tensor(T[xt][:, 4 * a:4 * b], T.h[:, 0:1152].indirect(T[arr][:, 36 * hf:36 * hf + 36]), T.zt[:, 4 * a:4 * b], A.add),
-              lanes("h") + [R(arr), R("zt", a, b)], [R(xt, a, b)])
-        new_half(0)
-        scan(("soc", 0, 288), ("mask16", 0, 288), ("cs", 0, 288))
+        if last:
+            new_part(0)
+            change_scan()
         quant_x(r + 1, 0)
-        ts(("c01", 0, 18), ("soc", 15, 288, 16), 0.0, None, A.is_gt)
-        new_half(1)
+        if last:
+            change()
+            new_part(1)
+        else:
+            score_part(r + 1, 0)
+            new_part(1)
+            change_scan()
+            quant_x(r + 1, 1)
+            change()
+            score_part(r + 1, 1)
+            idsg_part(0)
         tt(("m2", 0, 18), ("dd", 0, 18), ("c01", 0, 18), A.mult)
         tt(("m2", 18, 36), ("dd", 18, 36), ("c01", 0, 18), A.mult)
-        quant_x(r + 1, 1)
+        if last:
+            quant_x(r + 1, 1)
         tt(("ab", 0, 36), ("ab", 0, 36), ("m2", 0, 36), A.add)
-        if r < 2:
-            score_half(r + 1, 0)
-            idsg_half(0)
-            cp(("lab", 0, 36), ("ab", 0, 36))
-            score_half(r + 1, 1)
-            idsg_half(1)
-        else:
-            cp(("lab", 0, 36), ("ab", 0, 36))
+        if not last:
+            idsg_part(1)
+        cp(("lab", 0, 36), ("ab", 0, 36))
 
     def out(q, dst, src, rd):
         op(q, lambda e: e.dma_start(dst, src), rd, [], dma=True)
     for hf in range(2):
-        mm(3 + hf, "v", 0, [R("qv")], "x3", hf * HC, hf * HC + HC)
+        mm(3 + hf, "v", 0, [R("qv")], "x3", *PART[hf])
     out("Y", T.oc[:, :], T.qx3[:, :].bitcast(dt.uint8), [R("qx3")])
     gather("S", ("opr", 0, C), ("idf", 0, C), ("sl", 0, 18))
-    V(lambda e: e.tensor_copy(T.yo[:, 0:HC], bank(3, HC)), [R("B3")], [R("yo", 0, HC)])
-    V(lambda e: e.tensor_copy(T.yo[:, HC:C], bank(4, HC)), [R("B4")], [R("yo", HC, C)])
+    for hf in range(2):
+        a, b = PART[hf]
+        V(lambda e: e.tensor_copy(T.yo[:, a:b], bank(3 + hf, b - a)), [R("B%d" % (3 + hf))], [R("yo", a, b)])
     gather("V", ("opr", C, 2 * C), ("idf", 0, C), ("lab", 0, 18))
     gather("S", ("opr", 2 * C, 3 * C), ("idf", 0, C), ("lab", 18, 36))
     out("Y", T.y[:, :], T.yo[:, :], [R("yo")])

from concourse.bass import DstId, RemoteDMATransfer
from concourse.mybir import dt, AluOpType, ActivationFunctionType

STEP = [4, 1, 2]
STAGES = 7
C = 288
HC = C // 2
PART = [(0, 160), (160, 288)]
MID = 336
K = 672
BIG = 2.0 ** 40
UP = 2.0 ** 36
TINY = -2.0 ** -100

SCRATCH = {"ps": ("psum", [128, 4096], "float32")}


def _bufs(where, dtype, **cols):
    for k in cols:
        SCRATCH[k] = (where, [128, cols[k]], dtype)


_bufs("sbuf", "bfloat16", xin=1152, xt1=1152, xt2=1152, xt3=1152, ut=512, vt=512, ones=512, eb=2048, tm=304, tm4=288, ma=304, mb=304,
      mask16=304, mask4=288, enc=288, sg=288, idsg=288, cs=288, w=1344, r=320, so1=304, son=304, soc=288,
      tt=1152, tq=1152, zt=1152, zp=1152, h=1152)
for _n, _c in [("u", 128), ("ur", 128), ("v", 128), ("w", 512), ("e", 512), ("z", 288), ("h", 288)] + [("x%d" % _r, 288) for _r in range(4)] + [("l%d" % _r, 288) for _r in range(3)]:
    SCRATCH["q" + _n] = ("sbuf", [128, _c], "float8_e4m3fn_x4")
    SCRATCH["p" + _n] = ("sbuf", [128, _c], "uint8")
_bufs("sbuf", "int32", pi=8, pk=8, offui=8, tai=18, tbi=18, sti=18)
_bufs("sbuf", "float32", pf=8, sc16=8, kp=8, sc4=8, revf=20, idf=288, ab=36, dd=36, m2=36, c01=18, za=20, tmp=20, yy=20,
      wl=1344, rl=304, so4=288, sol=304, opr=864, yo=288)
_bufs("sbuf", "uint16", offu=8, rev=20, sl=20, lab=36, off=20, own0=72, own1=72, own2=72, arr0=72, arr1=72, arr2=72)

DMAS = ["d%d" % _i for _i in range(20)]
SEMAPHORES = ["cV", "cS", "cT", "cP", "left"] + ["ax%d" % _r for _r in range(3)] + ["al%d" % _r for _r in range(3)] + DMAS


def make_tracker(g, T):
    queues = {"V": g.vector, "S": g.scalar, "T": g.tensor, "P": g, "Y": g.sync}
    csem = {"V": "cV", "S": "cS", "T": "cT", "P": "cP"}
    count = {}
    known = {q: {} for q in queues}
    clocks = {}
    writes, reads = {}, {}
    ndma = [0]

    def wait(q, toks):
        best = {}
        for s, v in toks:
            if known[q].get(s, 0) < v:
                best[s] = max(best.get(s, 0), v)
        items = sorted(best.items())
        for s, v in items:
            if not any(o[0] != s and clocks[o].get(s, 0) >= v for o in items):
                queues[q].wait_ge(T.sem[s], v)
        for s, v in items:
            for s2, v2 in clocks[(s, v)].items():
                known[q][s2] = max(known[q].get(s2, 0), v2)
            known[q][s] = max(known[q].get(s, 0), v)

    def deps(q, rd, wr):
        toks = []
        for k, a, b in rd + wr:
            toks += [t for x, y, t, oq in writes.get(k, []) if x < b and a < y]
        for k, a, b in wr:
            toks += [t for x, y, t, oq in reads.get(k, []) if x < b and a < y and (oq != q or k in ("w", "wl"))]
        return toks

    def note(q, rd, wr, tok):
        for k, a, b in wr:
            writes[k] = [e for e in writes.get(k, []) if not (a <= e[0] and e[1] <= b)] + [(a, b, tok, q)]
            reads[k] = [e for e in reads.get(k, []) if not (a <= e[0] and e[1] <= b)]
        for k, a, b in rd:
            reads.setdefault(k, []).append((a, b, tok, q))

    def op(q, call, rd, wr, dma=False):
        wait(q, deps(q, rd, wr))
        s, inc = csem.get(q), 1
        if dma:
            s, inc = DMAS[ndma[0]], 16
            ndma[0] += 1
        count[s] = count.get(s, 0) + inc
        tok = (s, count[s])
        call(queues[q]).then_inc(T.sem[s], inc)
        clocks[tok] = dict(known[q])
        clocks[tok][s] = count[s]
        note("dma" if dma else q, rd, wr, tok)

    def arrival(s, v, wr):
        clocks[(s, v)] = {s: v}
        count[s] = v
        note("net", [], wr, (s, v))

    def before(q, rd):
        wait(q, deps(q, rd, []))

    def finish():
        for s in sorted(count):
            g.wait_ge(T.sem[s], count[s])

    return op, arrival, before, finish, count


def rank_program(g, core, T, topo):
    rank = T.rank_of(core)
    if rank is None:
        return
    A = AluOpType
    F = ActivationFunctionType
    op, arrival, before, finish, count = make_tracker(g, T)

    def R(k, a=0, b=100000):
        return (k, a, b)

    def lanes(k, a=0, b=C):
        return [(k + "_" + str(t), a, b) for t in range(4)]

    def V(call, rd, wr):
        op("V", call, rd, wr)

    def S(call, rd, wr):
        op("S", call, rd, wr)

    def ap(x):
        if not isinstance(x, tuple):
            return x
        return T[x[0]][:, x[1]:x[2]:x[3]] if len(x) > 3 else T[x[0]][:, x[1]:x[2]]

    def rgs(*xs):
        return [(x[0], x[1], x[2]) for x in xs if isinstance(x, tuple)]

    def ts(out, in0, s1, s2, *ops):
        V(lambda e: e.tensor_scalar(ap(out), ap(in0), ap(s1), ap(s2), *ops), rgs(in0, s1, s2), rgs(out))

    def tt(out, in0, in1, o):
        V(lambda e: e.tensor_tensor(ap(out), ap(in0), ap(in1), o), rgs(in0, in1), rgs(out))

    def cp(out, in_):
        V(lambda e: e.tensor_copy(ap(out), ap(in_)), rgs(in_), rgs(out))

    def act(out, in_, fn, **k):
        S(lambda e: e.activation(ap(out), ap(in_), fn, **{x: ap(k[x]) for x in k}), rgs(in_, *k.values()), rgs(out))

    def gather(q, out, win, off, wr=None, rd=None):
        rr, ww = rgs(off) + (rd if rd else rgs(win)), wr if wr else rgs(out)
        if q == "V":
            V(lambda e: e.tensor_copy(ap(out), ap(win).indirect(ap(off))), rr, ww)
        else:
            S(lambda e: e.activation(ap(out), ap(win).indirect(ap(off)), F.Copy), rr, ww)

    def iota(out, pat, base, cm, flag=True):
        if flag:
            op("P", lambda e: e.iota(ap(out), pat, base, cm, allow_small_or_imprecise_dtypes=True), [], rgs(out))
        else:
            op("P", lambda e: e.iota(ap(out), pat, base, cm), [], rgs(out))

    def quant(q, a, b, src, rd):
        V(lambda e: e.quantize_mx(T["q" + q][:, a:b], T["p" + q][:, a:b], T[src][:, 4 * a:4 * b]), rd, [R("q" + q, a, b)])

    def load(q, dst, src, key, a=0, b=100000):
        op(q, lambda e: e.dma_start(dst, src), [], [(key, a, b)], dma=True)

    def load_x(a, b):
        load("Y", T.xin[:, 4 * a:4 * b], T.x[:, 4 * a:4 * b], "xin", a, b)
    load_x(*PART[0])
    load("S", T.ut[:, :], T.u[:, :], "ut")
    load_x(*PART[1])
    load("Y", T.sti[:, :], T.st[:, :], "sti")
    load("S", T.tai[:, :], T.ta[:, :], "tai")
    load("S", T.tbi[:, :], T.tb[:, :], "tbi")
    load("Y", T.qw[:, :].bitcast(dt.uint8), T.wc[:, :], "qw")
    load("Y", T.pw[:, :], T.ws[:, :], "pw")
    load("Y", T.vt[:, :], T.v[:, :], "vt")

    def unpacker(b):
        op("P", lambda e: e.affine_select(T.eb[:, 512 * b:512 * b + 512], T.ones[:, :], [[1, 512]], A.is_equal, 0.0, -b, -4), [R("ones", 0, 512)], [R("eb", b, b + 1)])

    iota(("pi", 0, 5), [[1, 5]], 0, 1, False)
    iota(("offui", 0, 8), [[16, 8]], 0, 0, False)
    iota(("tm", 0, 304), [[0, 19], [1, 16]], 0, 0)
    iota(("revf", 0, 20), [[-16, 20]], 320, 0)
    iota(("enc", 0, 256), [[1, 256]], 1, 0)
    iota(("enc", 256, 288), [[2, 32]], 258, 0)
    iota(("tm4", 0, 288), [[0, 72], [1, 4]], 0, 0)

    def fill(win, a, b):
        act((win, a, b), ("ones", 0, b - a), F.Copy)

    V(lambda e: e.memset(T.ones[:, :], 1.0), [], [R("ones", 0, 512)])
    V(lambda e: e.memset(T.r[:, 304:320], 1.0), [], [R("r", 304, 320)])
    for a in (0, 448, 896):
        fill("w", a, a + 448)
    unpacker(0)
    unpacker(1)
    for j, (src, sh, an) in enumerate([(0, 0, 15), (1, 0, 15), (0, 2, 3), (0, 0, 3)]):
        if sh:
            ts(("pk", j, j + 1), ("pi", src, src + 1), sh, an, A.arith_shift_right, A.bitwise_and)
        else:
            ts(("pk", j, j + 1), ("pi", src, src + 1), an, None, A.bitwise_and)
    cp(("offu", 0, 8), ("offui", 0, 8))
    cp(("pf", 0, 4), ("pk", 0, 4))
    p16, q16, p4, t4 = [("pf", j, j + 1) for j in range(4)]
    ts(("ma", 0, 304), ("tm", 0, 304), q16, BIG, A.is_equal, A.mult)
    ts(("mb", 0, 304), ("tm", 0, 304), p16, None, A.not_equal)
    ts(("sc16", 0, 1), p16, 15.0, 1.0 / BIG, A.is_equal, A.max)
    ts(("kp", 1, 2), p16, 15.0, K * BIG, A.not_equal, A.mult)
    tt(("mask16", 0, 304), ("ma", 0, 304), ("mb", 0, 304), A.max)
    ts(("revf", 0, 20), ("revf", 0, 20), p16, None, A.subtract)
    ts(("kp", 0, 1), ("kp", 1, 2), float(K), None, A.max)
    quant("u", 0, 128, "ut", [R("ut")])
    cp(("rev", 0, 20), ("revf", 0, 20))
    V(lambda e: e.tensor_copy(T.qur[:, 0:128].bitcast(dt.uint32), T.qu[:, 0:128].bitcast(dt.uint32).indirect(T.offu[:, 0:8])), [R("qu"), R("offu")], [R("qur", 0, 1)])
    S(lambda e: e.activation(T.pur[:, 0:128], T.pu[:, 0:128].indirect(T.offu[:, 0:8]), F.Copy), [R("qu"), R("offu")], [R("qur", 1, 2)])

    def quant_x(r, hf):
        src = "xt%d" % r if r else "xin"
        a, b = PART[hf]
        quant("x%d" % r, a, b, src, [R(src, a, b)])

    def bank(i, n):
        return T.ps[:, 512 * i:512 * i + n]

    def mm(i, st, sa, stk, mv, a, b):
        op("T", lambda e: e.matmul_mx(bank(i, b - a), T["q" + st][:, sa:sa + 128], T["p" + st][:, sa:sa + 128], T["q" + mv][:, a:b], T["p" + mv][:, a:b], True, True),
           stk + [R("q" + mv, a, b)], [R("B%d" % i)])

    ukeys = [R("qur", 0, 2)]

    def score_part(r, hf):
        a, b = PART[hf]
        mm(hf, "ur", 0, ukeys, "x%d" % r, a, b)
        S(lambda e: e.activation(T.sg[:, a:b], bank(hf, b - a), F.Sign, bias=TINY), [R("B%d" % hf)], [R("sg", a, b)])

    def idsg_part(hf):
        a, b = PART[hf]
        tt(("idsg", a, b), ("sg", a, b), ("enc", a, b), A.mult)

    def scan(out, mask, row):
        V(lambda e: e.tensor_tensor_scan(ap(out), ap(mask), ap(row), 0.0, A.mult, A.add), rgs(mask, row), rgs(out))

    def table(q, dst, src, first, c, d):
        m, o = (MID, 0) if first else (MID + K, 18)
        if c == 16:
            gather(q, (dst, m + 258, m + 321, 2), (src, 0, C), ("lab", o + c, o + d))
        else:
            gather(q, (dst, m + 1 + 16 * c, m + 1 + 16 * d), (src, 0, C), ("lab", o + c, o + d))

    def mirror(win, first):
        m = MID if first else MID + K
        gather("S", (win, m - 320, m), (win, m, m + 336), ("rev", 0, 20))

    VC = 10

    def stage_gather(t):
        row, win, off = "r", ("w", 0, 2 * K), "off"
        if t == 0:
            win, off = ("idsg", 0, C), "sl"
        elif t == STAGES:
            row, win = "rl", ("wl", 0, 2 * K)
        gather("V", (row, 0, 16 * VC), win, (off, 0, VC))
        gather("S", (row, 16 * VC, 304), win, (off, VC, 19))

    M16, M4, SC16, SC4 = ("mask16", 0, 304), ("mask4", 0, 288), ("sc16", 0, 1), ("sc4", 4, 5)

    def own_scan():
        scan(("so1", 0, 304), M16, ("r", 0, 304))

    def next_scan():
        scan(("son", 0, 304), M16, ("r", 1, 305))

    def nothing():
        pass

    def unsigned_list(scalar=nothing, vector=nothing, between=nothing):
        own_scan()
        next_scan()
        scalar()
        act(("za", 0, 19), ("so1", 15, 304, 16), F.Abs, scale=SC16)
        vector()
        ts(("tmp", 0, 19), ("son", 15, 304, 16), 0.0, float(K), A.is_gt, A.mult)
        between()
        tt(("yy", 0, 19), ("za", 0, 19), ("tmp", 0, 19), A.add)

    def unsigned_end():
        ts(("off", 0, 19), ("yy", 0, 19), float(MID), None, A.add)

    def signed_list(between=nothing):
        next_scan()
        own_scan()
        ts(("tmp", 0, 19), ("son", 15, 304, 16), 0.0, ("kp", 0, 1), A.is_gt, A.mult)
        between()
        tt(("yy", 0, 19), ("so1", 15, 304, 16), ("tmp", 0, 19), A.add)
        ts(("off", 0, 19), ("yy", 0, 19), SC16, float(MID), A.mult, A.add)

    def unpack_lane(mv, i, b):
        mm(i, "e", 128 * b, [R("qe", 128 * b, 128 * b + 128)], mv, 0, C)

    def piece(q, buf, i, b, hf):
        a = hf * HC
        out, src = T[buf][:, 4 * a + b:4 * (a + HC):4], T.ps[:, 512 * i + a:512 * i + a + HC]
        rd, wr = [R("B%d" % i)], [(buf + "_" + str(b), a, a + HC)]
        if q == "V":
            V(lambda e: e.tensor_copy(out, src), rd, wr)
        else:
            S(lambda e: e.activation(out, src, F.Copy), rd, wr)

    cp(("sl", 0, 18), ("sti", 0, 18))
    cp(("sl", 18, 19), ("sti", 0, 1))
    quant_x(0, 0)
    quant_x(0, 1)
    score_part(0, 0)
    score_part(0, 1)
    cp(("lab", 0, 18), ("tai", 0, 18))
    cp(("lab", 18, 36), ("tbi", 0, 18))
    idsg_part(0)
    idsg_part(1)

    def sc4_factor(k):
        ts(("sc4", k, k + 1), p4, k + 1.0, 1.0 / UP, A.is_ge, A.max)

    def later(t):
        if t == 2:
            ts(M4, ("tm4", 0, 288), p4, UP, A.not_equal, A.mult)
        elif t == 3:
            sc4_factor(0)
            sc4_factor(1)
        elif t == 4:
            sc4_factor(2)
            tt(("sc4", 3, 4), ("sc4", 0, 1), ("sc4", 1, 2), A.mult)
        elif t == 5:
            ts(SC4, ("sc4", 3, 4), ("sc4", 2, 3), 4.0, A.mult, A.mult)

    def differences():
        tt(("dd", 0, 18), ("ab", 18, 36), ("ab", 0, 18), A.subtract)
        tt(("dd", 18, 36), ("ab", 0, 18), ("ab", 18, 36), A.subtract)

    for r in range(3):
        partner = T.cores[rank ^ STEP[r]]
        rid, pid = topo.addr(partner, core)
        engines = topo.engines(core, partner)[:8]
        mask = sum(1 << e for e in engines)
        ne = len(engines)
        qx, lx, own, arr = "x%d" % r, "l%d" % r, "own%d" % r, "arr%d" % r
        own_t, got_t = [2, 3, 4, 5], [6, 7, 0, 1]

        before("P", [R("q" + qx)])
        g.remote_dma(T["q" + lx][:, :].bitcast(dt.uint8), T["q" + qx][:, :].bitcast(dt.uint8), T.sem["ax%d" % r], T.sem.left, pid, rid, mask)
        g.remote_dma(T["p" + lx][:, :], T["p" + qx][:, :], T.sem["ax%d" % r], T.sem.left, pid, rid, mask)
        count["left"] = count.get("left", 0) + 2 * ne
        arrival("ax%d" % r, 2 * ne, [R("q" + lx)])
        arrival("al%d" % r, ne, [R(arr)])
        if r == 0:
            iota(("idf", 0, 288), [[1, 288]], 0, 0)
            unpacker(2)
            unpacker(3)

        def tails():
            table("S", "w", "idsg", True, 16, 18)
            table("S", "w", "idsg", False, 16, 18)
        stage_gather(0)
        unsigned_list(tails, lambda: table("V", "w", "idsg", False, 0, 6))
        table("S", "w", "idsg", True, 0, 16)
        table("S", "w", "idsg", False, 12, 16)
        table("V", "w", "idsg", False, 6, 12)
        unsigned_end()
        if r:
            for b in range(4):
                unpack_lane(qx, own_t[b], b)
            for b in range(4):
                unpack_lane(lx, got_t[b], b)
        own_p = [(b, hf) for b in range(4) for hf in range(2)]

        def own_pieces(n):
            for i in range(n):
                b, hf = own_p.pop(0)
                piece("S", "tt", own_t[b], b, hf)

        def plain_tails():
            table("S", "wl", "idf", True, 16, 18)
            table("S", "wl", "idf", False, 16, 18)

        for t in range(1, STAGES):
            stage_gather(t)
            mine = nothing
            if r == 0:
                mine = lambda: later(t)
                if t == 1:
                    cp(("ab", 0, 18), ("tai", 0, 18))
                    cp(("ab", 18, 36), ("tbi", 0, 18))
                elif t <= 5:
                    b = t - 2
                    quant("e", 128 * b, 128 * b + 128, "eb", [R("eb", b, b + 1)])
                    unpack_lane(qx, own_t[b], b)
                    if b == 3:
                        for b in range(4):
                            unpack_lane(lx, got_t[b], b)
            if t == 1:
                unsigned_list(nothing if r else lambda: fill("wl", 0, 336))
                unsigned_end()
                mirror("w", True)
            elif t == 2:
                mirror("w", False)
                if r == 0:
                    fill("wl", 336, 672)
                signed_list(mine)
                differences()
            elif t == 6 and r == 0:
                unsigned_list(lambda: own_pieces(2))
                own_pieces(2)
                unsigned_end()
            else:
                if t < 5:
                    if r == 0:
                        fill("wl", 336 * t - 336, 336 * t)
                    table("S", "wl", "idf", t == 3, 0, 16)
                elif r:
                    mirror("wl", t == 5)
                if t == (4 if r else 5):
                    plain_tails()
                if t == 5 or r and t != 4:
                    own_pieces(2)
                signed_list(mine)
        stage_gather(STAGES)
        own_pieces(2)
        scan(("so4", 0, 288), M4, ("rl", 0, 288))
        ts((own, 0, 72), ("so4", 3, 288, 4), SC4, t4, A.mult, A.add)
        before("P", [R(own)])
        g.remote_dma(T[arr][:, :], T[own][:, :], T.sem["al%d" % r], T.sem.left, pid, rid, mask)
        count["left"] += ne

        gather("S", ("zt", 576, 1152), ("tt", 0, 1152), (own, 36, 72), [R("zt", HC, C)], lanes("tt"))
        scan(("sol", 0, 304), M16, ("rl", 0, 304))
        gather("V", ("zt", 0, 576), ("tt", 0, 1152), (own, 0, 36), [R("zt", 0, HC)], lanes("tt"))
        ts(("sl", 0, 18), ("sol", 15, 288, 16), SC16, None, A.mult)
        ts(("sl", 18, 19), ("sol", 15, 16), SC16, None, A.mult)
        for hf in range(2):
            for b in (0, 1):
                piece("S", "tq", got_t[b], b, hf)
                piece("V", "tq", got_t[b + 2], b + 2, hf)
        if r == 0:
            quant("v", 0, 128, "vt", [R("vt")])

        for hf in range(2):
            a, b = PART[hf]
            m = (a + b) // 2
            gather("V", ("zp", 4 * a, 4 * m), ("tq", 0, 1152), (arr, a // 4, m // 4), [R("zp", a, m)], lanes("tq"))
            gather("S", ("zp", 4 * m, 4 * b), ("tq", 0, 1152), (arr, m // 4, b // 4), [R("zp", m, b)], lanes("tq"))
            quant("z", a, b, "zp", [R("zp", a, b)])
            for k in (0, 2, 1, 3):
                mm(4 * hf + k, "w", 128 * k, [R("qw"), R("pw")], "z", a, b)
        for hf in range(2):
            a, b = PART[hf]
            for k in (0, 2, 1, 3):
                i = 4 * hf + k
                out, wr = T.h[:, 4 * a + k:4 * b:4], [("h_%d" % k, a, b)]
                if k < 2:
                    V(lambda e: e.tensor_scalar(out, bank(i, b - a), 0.03125, None, A.mult), [R("B%d" % i)], wr)
                else:
                    S(lambda e: e.activation(out, bank(i, b - a), F.Copy, scale=0.03125), [R("B%d" % i)], wr)

        xt, last = "xt%d" % (r + 1), r == 2

        def new_part(hf):
            a, b = PART[hf]
            V(lambda e: e.tensor_tensor(T[xt][:, 4 * a:4 * b], T.h[:, 0:1152].indirect(T[arr][:, a // 4:b // 4]), T.zt[:, 4 * a:4 * b], A.add),
              lanes("h") + [R(arr), R("zt", a, b)], [R(xt, a, b)])

        def change_scan():
            scan(("soc", 0, 288), ("mask16", 0, 288), ("cs", 0, 288))

        def change():
            ts(("c01", 0, 18), ("soc", 15, 288, 16), 0.0, None, A.is_gt)
        if not last:
            new_part(0)
        quant("h", 0, C, "h", lanes("h"))
        mm(2, "ur", 0, ukeys, "h", 0, C)
        S(lambda e: e.activation(T.cs[:, :], bank(2, C), F.Sign, bias=TINY), [R("B2")], [R("cs", 0, C)])
        if last:
            new_part(0)
            change_scan()
        quant_x(r + 1, 0)
        if last:
            change()
            new_part(1)
        else:
            score_part(r + 1, 0)
            new_part(1)
            change_scan()
            quant_x(r + 1, 1)
            change()
            score_part(r + 1, 1)
            idsg_part(0)
        tt(("m2", 0, 18), ("dd", 0, 18), ("c01", 0, 18), A.mult)
        tt(("m2", 18, 36), ("dd", 18, 36), ("c01", 0, 18), A.mult)
        if last:
            quant_x(r + 1, 1)
        tt(("ab", 0, 36), ("ab", 0, 36), ("m2", 0, 36), A.add)
        if not last:
            idsg_part(1)
        cp(("lab", 0, 36), ("ab", 0, 36))

    def out(q, dst, src, rd):
        op(q, lambda e: e.dma_start(dst, src), rd, [], dma=True)
    for hf in range(2):
        mm(3 + hf, "v", 0, [R("qv")], "x3", *PART[hf])
    out("Y", T.oc[:, :], T.qx3[:, :].bitcast(dt.uint8), [R("qx3")])
    gather("S", ("opr", 0, C), ("idf", 0, C), ("sl", 0, 18))
    for hf in range(2):
        a, b = PART[hf]
        V(lambda e: e.tensor_copy(T.yo[:, a:b], bank(3 + hf, b - a)), [R("B%d" % (3 + hf))], [R("yo", a, b)])
    gather("V", ("opr", C, 2 * C), ("idf", 0, C), ("lab", 0, 18))
    gather("S", ("opr", 2 * C, 3 * C), ("idf", 0, C), ("lab", 18, 36))
    out("Y", T.y[:, :], T.yo[:, :], [R("yo")])
    for k in range(4):
        out("S" if k % 2 else "Y", T.osc[4 * k:4 * k + 4, :], T.px3[32 * k:32 * k + 4, :], [R("qx3")])
    out("S", T.op[:, :], T.opr[0:128:16, :], [R("opr")])
    finish()
